import numpy as np, ml_dtypes
CORES = [40,41,42,43,44,45,46,47]
N = 8
BF = ml_dtypes.bfloat16
def gentries(a):
    return np.ascontiguousarray(a.reshape(8, 16, -1).transpose(0, 2, 1)).reshape(8, -1)
def gtable(e):
    e = np.asarray(e); return np.ascontiguousarray(e.reshape(8, -1, 16).transpose(0, 2, 1)).reshape(128, -1).astype(np.int32)
def f(rng, *shape):
    return (rng.standard_normal(shape, dtype=np.float32) * np.exp2(rng.integers(-2, 3, shape[:-1] + (1,)))).astype(BF)
def wide(rng, *shape):
    v = f(rng, *shape).astype(np.float32); k = shape[:-2] + (1, shape[-1])
    return (v * np.exp2(rng.integers(-6, 7, k)) * (rng.random(k) > 0.0625)).astype(BF)
W, C, LOOK, RO = 6144, 1024, 3, 4
def cuts(rng, least=3):
    room = W - least * C - W // 16
    e = np.sort(rng.integers(0, room + 1, C - 1))
    return least + np.diff(np.concatenate([np.array([0]), e, np.array([room])])).astype(np.int64)
def laid(rng, le, first):
    o = rng.permutation(C); o = np.concatenate([np.array([first]), o[o != first]])
    st = np.zeros(C, np.int64); st[o] = np.add.accumulate(le[o]) - le[o]
    return st
def walk(le):
    cyc = np.repeat(np.arange(C), le)
    return cyc, np.arange(cyc.size) - np.repeat(np.add.accumulate(le) - le, le)
def rings(s, order, st, le):
    cyc, off = walk(le); a, n = st[cyc], le[cyc]
    s[order[a + off]] = order[a + (off + 1) % n] + order[a + (off + n - 1) % n]
    return s, order[st], np.concatenate([order[st + 1], order[st + le - 1]])
def hang(rng, order, st, le, near, mix):
    kid = np.full(W, -1, np.int64)
    a, b = rng.permutation(np.arange(0, C, 2)), rng.permutation(np.arange(1, C, 2))
    m = np.array(a[:mix]); a[:mix] = b[:mix]; b[:mix] = m
    for par, kids in ((0, b), (1, a)):
        i = np.arange(par, C, 2); w = st[i] + 1
        if not near: w = np.concatenate([w, st[i] + 2, (st[i] + 3)[le[i] > 3]])
        kid[order[rng.permutation(w)[:C // 2]]] = kids
    return kid
def skeleton(rng, near, far=()):
    out = []
    for g in range(N * 8):
        order = rng.permutation(W); le = cuts(rng, 5 if g in far else 3); st = laid(rng, le, int(rng.integers(0, C)))
        s, r, e = rings(rng.integers(1, 2 * W - 2, W), order, st, le); tight = near and g % 2 == 1 and g not in far
        out.append((s, r, e, hang(rng, order, st, le, tight, 0 if tight else C // 8)))
    return out
def items(rng):
    a = np.exp2(rng.integers(-2, 3, (N, 128, 1))).astype(np.float32)
    x = rng.standard_normal((N, 128, W), dtype=np.float32) * a
    h = np.repeat(rng.choice(np.array([-0.7, -0.4, -0.1, 0.2], np.float32), (N, 8, RO * C)), 16, axis=1)
    return x, (np.float32(0.7) * rng.standard_normal((N, 128, RO * C), dtype=np.float32) + h) * a
def pat(rng, u):
    m = rng.choice(np.array([1, 3, 5, 7]), u.shape); sh = rng.integers(0, 16, u.shape)
    return ((np.arange(16)[:, None] * m + sh) & 15) < u
def pack(x, q, out):
    s, r, e, k = [np.stack(a) for a in zip(*out)]
    return {"x": np.ascontiguousarray(x.reshape(N, 128, W)).astype(BF), "nsum": s.reshape(N, 8, W).astype(np.int32), "rho": np.stack([gtable(a) for a in r.reshape(N, 8, C)]),
            "nei": np.stack([gtable(a) for a in e.reshape(N, 8, 2 * C)]), "kid": k.reshape(N, 8, W).astype(np.int32), "dem": np.ascontiguousarray(q.reshape(N, 128, RO * C)).astype(BF)}
def setup_inputs(rng):
    x, q = items(rng)
    return pack(x, q, skeleton(rng, False))
def setup_inputs_corners(rng):
    out = []; fit = np.zeros((N * 8, W), bool)
    for g in range(N * 8):
        if g % 8 == 0: modes = rng.permutation(8)
        mode = int(modes[g % 8]); order = rng.permutation(W)
        le = rng.choice(np.array([3, 4, LOOK + 1, LOOK + 2, 2 * LOOK, 2 * LOOK + 1, 2 * LOOK + 2]), C).astype(np.int64)
        le = np.where(np.add.accumulate(le - 3) > W - 3 * C, 3, le)
        if g % 2 == 1: le[rng.integers(0, C)] += W - np.sum(le)
        st = laid(rng, le, int(rng.integers(0, C))); s, r, e = rings(rng.integers(1, 2 * W - 2, W), order, st, le)
        cyc, p = walk(le); k = rng.choice(np.array([0, 0, 1, 2, 3, 4, 5, 5, 6, 6]), C)[cyc]; n = le[cyc]; back = n - p
        fit[g] = rng.random(W) < 0.5
        fit[g, order[st[cyc] + p]] = (p == 0) | ((k == 0) & ((p == LOOK) | (back == LOOK))) | ((k == 1) & ((p == LOOK + 1) | (back == 1))) | ((k == 2) & (p == n // 2)) | (k == 4) | ((k == 5) & ((p == 1) | (back == 1))) | ((k == 6) & (rng.random(p.size) < 0.5))
        kid = np.full(W, -1, np.int64)
        if mode == 0: kid[order[st + 1]] = (np.arange(C) + 1) % C
        elif mode == 2: kid[order[st]] = rng.permutation(C)
        elif mode == 3: kid[order[st + 1]] = np.arange(C)
        elif mode >= 4: kid = hang(rng, order, st, le, mode < 6, 0 if mode < 6 else C // 8)
        out.append((s, r, e, kid))
    fit = fit.reshape(N, 8, 1, W)
    u = np.where(fit, rng.choice(np.array([9, 16]), fit.shape), rng.choice(np.array([0, 8]), fit.shape))
    x = np.where(pat(rng, u), np.float32(1), np.float32(-1)) * (2 + rng.random((N, 8, 16, W), dtype=np.float32))
    q = 2 * rng.random((N, 8, 16, RO * C), dtype=np.float32) - 1
    return pack(x, q + rng.choice(np.array([0, 8, -8], np.float32), (N, 8, 1, RO * C), p=[0.8, 0.1, 0.1]), out)
def setup_inputs_crowd(rng):
    x, q = items(rng); q = q.reshape(N, 8, 16, RO, C); xv = x.reshape(N * 8, 16, W)
    h = int(rng.integers(0, 8)); k = (h + 1) % 8; deep = []
    for r in range(N):
        for t in range(RO):
            o = rng.permutation(8); i = rng.choice(np.array([0, C - 1, C // 2, C // 2 + 1]), 2)
            if t == 0:
                o = o[(o != h) & (o != k)]
                if r == 0:
                    j = int(np.argmax(o % 2)); o[[1, j]] = o[[j, 1]]
                o = np.concatenate([np.array([h]), o]); deep.append(r * 8 + int(o[4])); q[r, o[4], :, 0] = -72
            q[r, o[0], :, t] = 128; q[r, o[1], :, t] = 128; q[r, o[1], :, t, i[0]] = -128
            q[r, o[2], :, t] = -128; q[r, o[3], :, t] = -128; q[r, o[3], :, t, i[1]] = 128
    q[:, k, :, 0, C - 1] = 128; q[:, k, :, 1, C - 1] = -72
    out = skeleton(rng, True, set(deep) | set(r * 8 + k for r in range(N)))
    for r in range(N):
        for g, e in ((deep[r], np.arange(2 * C)), (r * 8 + k, np.array([C - 1, 2 * C - 1]))):
            a = out[g][2][e]; b = out[g][0][a] - out[g][1][e % C]
            xv[g][:, a] -= 96; xv[g][:, b] -= 48
    return pack(x, q, out)
def setup_inputs_ends(rng):
    zig = np.zeros(W, np.int64); zig[0::2] = np.arange(W // 2); zig[1::2] = W - 1 - np.arange(W // 2)
    out = []
    for g in range(N * 8):
        order = zig if g % 2 == 0 else W - 1 - zig; first = C - 1 if (g // 2) % 2 == 1 else 0
        le = cuts(rng); le[first] = max(int(le[first]), 5); st = laid(rng, le, first)
        s, r, e = rings(rng.choice(np.array([1, 2 * W - 3]), W), order, st, le)
        out.append((s, r, e, hang(rng, order, st, le, False, C // 8)))
    u = rng.choice(np.array([0, 8, 9, 16]), (N, 8, 1, W), p=[0.15, 0.25, 0.35, 0.25])
    u[:, 0::2, 0, 0] = 8; u[:, 0::2, 0, W - 1] = 9; u[:, 1::2, 0, 0] = 9; u[:, 1::2, 0, W - 1] = 8
    m = rng.choice(np.array([0, 8, 16]), (N, 8, 1, RO * C), p=[0.15, 0.25, 0.6])
    for g in range(N * 8):
        if (g // 2) % 2 == 0:
            s, r, e, kd = out[g]; a = int(e[0]); b = int(s[a] - r[0]); c = int(s[b] - a)
            u[g // 8, g % 8, 0, a] = 8; u[g // 8, g % 8, 0, b] = 8; u[g // 8, g % 8, 0, c] = 9; u[g // 8, g % 8, 0, int(e[C])] = 9
            kd[r[0]] = kd[a]; kd[a] = -1
            m[g // 8, g % 8, 0, 0] = 0; m[g // 8, g % 8, 0, C] = 16
    return pack(np.where(pat(rng, u), np.float32(1024), np.float32(-1024)), np.where(pat(rng, m), np.float32(1024), np.float32(-1024)), out)
def setup_inputs_spread(rng):
    return pack(wide(rng, N, 128, W), wide(rng, N, 128, RO * C), skeleton(rng, False))
def setup_inputs_ties(rng):
    a = np.exp2(rng.integers(-2, 3, (1, 1, 16, 1))).astype(np.float32)
    m = rng.integers(0, 4, (N, 8, 16, W)); k = rng.integers(0, 4, (N, 8, 16, RO * C)) + rng.choice(np.array([0, 0, 1]), (N, 8, 1, RO * C))
    return pack(a * (1 + m * np.float32(0.0078125)), a * (1 + k * np.float32(0.0078125)), skeleton(rng, False))
def check_inputs(d):
    bad = []
    for k, lo, hi in (("nsum", 1, 2 * W - 3), ("rho", 0, W - 1), ("nei", 0, W - 1), ("kid", -1, C - 1)):
        if np.min(d[k]) < lo or np.max(d[k]) > hi: bad.append("range of " + k)
    for k in ("x", "dem"):
        a = np.abs(d[k].astype(np.float32))
        if not np.all(np.isfinite(a)): bad.append("numbers of " + k + " finite")
        if np.any((a > 0) & (a < 2.0 ** -126)): bad.append("no subnormal number in " + k)
    kd = np.sort(d["kid"].reshape(N * 8, W), axis=1)
    if np.any((kd[:, 1:] == kd[:, :-1]) & (kd[:, 1:] >= 0)): bad.append("no lane twice in a row of kid")
    if bad: return bad
    s = d["nsum"].astype(np.int64).reshape(-1)
    ro = np.stack([gentries(a) for a in d["rho"]]).astype(np.int64).reshape(-1)
    ne = np.stack([gentries(a) for a in d["nei"]]).astype(np.int64).reshape(N * 8, 2, C)
    cur, last = ne[:, 0].reshape(-1), ne[:, 1].reshape(-1); base = np.repeat(np.arange(N * 8) * W, C); prev = ro
    seen = np.zeros(N * 8 * W, np.int64); np.add.at(seen, base + ro, 1)
    good = bool(np.max(seen) == 1 and np.all(s[base + ro] == cur + last) and np.all(cur != last))
    while good and cur.size:
        at = base + cur; np.add.at(seen, at, 1); nx = s[at] - prev; home = nx == ro
        good = not (np.any(seen[at] > 1) or np.any(nx < 0) or np.any(nx >= W) or np.any(home & (cur != last)))
        go = ~home; prev, cur, ro, last, base = cur[go], nx[go], ro[go], last[go], base[go]
    if not good: bad.append("cycles whole and apart")
    return bad
def reach(a, b):
    return np.sum((a >= b).astype(np.int64), axis=-2) >= 9
def reference(x, nsum, rho, nei, kid, dem):
    xs = x.astype(np.float32).reshape(N * 8, 16, W); s = nsum.astype(np.int64).reshape(N * 8, W); kd = kid.astype(np.int64).reshape(N * 8, W)
    ro = np.stack([gentries(a) for a in rho]).astype(np.int64).reshape(N * 8, C)
    ne = np.stack([gentries(a) for a in nei]).astype(np.int64).reshape(N * 8, 2, C)
    q = dem.astype(np.float32).reshape(N * 8, 16, RO, C); lane = np.arange(C)
    live = np.ones((N * 8, C), bool); z = q[:, :, 0]
    for t in range(RO):
        w, pv, emb = [], [], live
        for side in range(2):
            prev, cur = ro, ne[:, side] + 0; stop = ~live; hit = np.zeros((N * 8, C), bool)
            for k in range(LOOK):
                home = cur == ro; fit = reach(np.take_along_axis(xs, cur[:, None, :], 2), z) & ~home
                hit = hit | (fit & ~stop); go = ~(stop | fit | home); stop = ~go
                nxt = np.take_along_axis(s, cur, 1) - prev
                prev, cur = np.where(go, cur, prev), np.where(go, nxt, cur)
            w.append(cur); pv.append(prev); emb = emb & hit
        emb = emb & (w[0] != w[1])
        g, i = np.nonzero(emb)
        for side in range(2):
            s[g, w[side][g, i]] += ro[g, i] - pv[side][g, i]
            ne[g, side, i] = w[side][g, i]
        s[g, ro[g, i]] = w[0][g, i] + w[1][g, i]
        j = np.take_along_axis(kd, w[0], 1); jj = np.maximum(j, 0)
        g, i = np.nonzero(emb & (lane % 2 == t % 2) & (j >= 0) & (jj % 2 != lane % 2) & np.take_along_axis(emb, jj, 1))
        h = jj[g, i]; v = w[0][g, i]; b = s[g, v] - ro[g, i]
        c, d = ne[g, 0, h], ne[g, 1, h]
        keep = np.sum((xs[g, :, c] >= xs[g, :, d]).astype(np.int64), axis=1) >= 9
        c, d = np.where(keep, c, d), np.where(keep, d, c)
        s[g, v] += c - b
        s[g, c] += v - ro[g, h]
        s[g, d] += b - ro[g, h]
        s[g, b] += d - v
        live = live & True; live[g, h] = False
        if t < RO - 1:
            fl = np.roll((~emb).reshape(N, 8, C), 1, axis=0); zc = np.roll(z.reshape(N, 8, 16, C), 1, axis=0)
            fl = np.where(lane % 2 == 1, np.roll(fl, 1, axis=1), fl); zc = np.where(lane % 2 == 1, np.roll(zc, 1, axis=1), zc)
            z = np.where(fl[:, :, None, :], zc, q[:, :, t + 1].reshape(N, 8, 16, C)).reshape(N * 8, 16, C)
    return {"ys": s.reshape(N, 8, W).astype(np.float32), "yn": ne.reshape(N, 8, 2 * C).astype(np.float32), "yl": live.reshape(N, 8, C).astype(np.float32)}

@@ -1,0 +1,567 @@
+from concourse.mybir import AluOpType as OP, ActivationFunctionType as AF
+
+W, C, RO, HC = 6144, 1024, 4, 512
+M64, M32, M1 = 1.5 * 2.0 ** 29, 1.5 * 2.0 ** 28, 1.5 * 2.0 ** 23
+FS, FK = 12, 10
+BIG = 1000
+XA = 4096
+OFF = 128.0
+
+SCRATCH = {
+    "xs": ("sbuf", [128, W], "bfloat16"), "ws": ("sbuf", [128, W + 2048], "float32"), "ks": ("sbuf", [128, W], "bfloat16"),
+    "d0": ("sbuf", [128, C], "bfloat16"), "dz": ("sbuf", [128, 3 * 2048], "bfloat16"),
+    "zz": ("sbuf", [128, 8 * HC], "bfloat16"), "zr": ("sbuf", [128, 3 * HC], "bfloat16"),
+    "oi": ("sbuf", [128, 6 * 32], "uint16"),
+    "ns": ("sbuf", [128, 384], "int32"), "ki": ("sbuf", [128, 384], "int32"), "li": ("sbuf", [128, 192], "int32"),
+    "st": ("sbuf", [128, 4 * 384], "float32"), "sb": ("sbuf", [128, 2 * 384], "bfloat16"),
+    "lf": ("sbuf", [128, 14848], "float32"), "lb": ("sbuf", [128, 4096], "bfloat16"), "lu": ("sbuf", [128, 3328], "uint16"),
+    "gt": ("sbuf", [128, 2 * 5 * 1024 + 3072], "bfloat16"),
+    "vt": ("sbuf", [128, 1536 + 5 * 512], "float32"), "t1": ("sbuf", [128, C], "float32"),
+    "t2": ("sbuf", [128, C], "float32"), "tb": ("sbuf", [128, HC], "bfloat16"), "yo": ("sbuf", [128, 1024], "float32"),
+    "cb": ("sbuf", [128, 2304], "bfloat16"), "cf": ("sbuf", [128, 1920], "float32"), "ci": ("sbuf", [128, 8], "int32"),
+    "px": ("psum", [128, 2048], "float32"), "pe": ("psum", [128, 2048], "float32"),
+}
+NDMA = 44
+SEMAPHORES = ["V", "S", "P", "G", "sent"] + ["q%d" % i for i in range(NDMA)]
+
+CYC, GA, SC, FIX, LAT, PEC = 1.04, 1.56, 3.6, 40.0, 90.0, 0.6
+VPEN, SLACK, TRIES, AHEAD, URGE = 2.0, 120.0, 3500, 1, 10000.0
+GUESSES = [({"small": 1.0, "ga": 0.8, "sc": 0.6, "pe": 0.75, "o": 1.0}, -40.0, 60.0, 300.0),
+           ({"small": 1.0, "ga": 1.2, "sc": 1.5, "pe": 1.0, "o": 1.0}, -20.0, 150.0, 150.0),
+           ({"small": 1.0, "ga": 1.0, "sc": 0.8, "pe": 1.5, "o": 1.0}, 20.0, 120.0, 200.0)]
+
+
+def build(T, topo, core, nxt):
+    ops = []
+    top = {"lf": 0, "lb": 0, "lu": 0, "cb": 0, "cf": 0}
+    ptop = [0, 0, 0, 0]
+
+    def A(name, a, n, step=1):
+        end = a + (n - 1) * step + 1
+        cs = slice(a, end, step) if step > 1 else slice(a, end)
+        return (T[name][0:128, cs], name, a, end, n, step)
+
+    def sub(v, a, n, step=1):
+        return A(v[1], v[2] + a * v[5], n, step * v[5])
+
+    def new(name, n):
+        a = top[name]; top[name] = a + (n + 7) // 8 * 8
+        return A(name, a, n)
+
+    def F(n): return new("lf", n)
+    def B(n): return new("lb", n)
+    def U(n): return new("lu", n)
+    def lo(v): return sub(v, 0, 32)
+    def hi(v): return sub(v, 32, 32)
+
+    def P(bank, n):
+        if ptop[bank] + n > 512: ptop[bank] = 0
+        a = ptop[bank]; ptop[bank] = a + n
+        return A("pe", bank * 512 + a, n)
+
+    def add(alts, rd, wr, tag, kind="c", extra=None):
+        cls = "pe" if "P" in alts else "o" if kind != "c" or "G" in alts else extra or "small"
+        ops.append({"alts": alts, "rd": [v[1:4] for v in rd], "wr": [v[1:4] for v in wr], "tag": tag, "kind": kind, "x": extra, "cls": cls})
+
+    def wide2(*vs):
+        return all(v[1] in ("lb", "gt", "cb", "sb", "zz", "d0", "ks", "tb") for v in vs)
+
+    def vc(n, k=1.0): return FIX + max(64, n * k) * CYC
+
+    def ts(o, i, s1, s2, op0, op1=None, tag="ts"):
+        rd = [i] + [s for s in (s1, s2) if isinstance(s, tuple)]
+        a1 = s1[0] if isinstance(s1, tuple) else s1
+        a2 = s2[0] if isinstance(s2, tuple) else s2
+        if op1 is None: fn = lambda q: q.tensor_scalar(o[0], i[0], a1, None, op0)
+        else: fn = lambda q: q.tensor_scalar(o[0], i[0], a1, a2, op0, op1)
+        add({"V": (vc(o[4], 0.5 if wide2(o, i) else 1), fn)}, rd, [o], tag)
+        return o
+
+    def lin(o, i, scale, bias, tag="lin"):
+        add({"V": (vc(o[4]), lambda q: q.tensor_scalar(o[0], i[0], scale, bias, OP.mult, OP.add)),
+             "S": (vc(o[4]) + 30, lambda q: q.activation(o[0], i[0], AF.Identity, bias=bias, scale=scale))}, [i], [o], tag)
+        return o
+
+    def tt(o, a, b, op, tag="tt"):
+        k = 1 if "pe" in (a[1], b[1]) else 2
+        add({"V": (vc(o[4], k), lambda q: q.tensor_tensor(o[0], a[0], b[0], op))}, [a, b], [o], tag)
+        return o
+
+    def cp(o, i, tag="cp", flex=False):
+        alts = {"V": (vc(o[4], 0.5 if wide2(o, i) else 1), lambda q: q.tensor_copy(o[0], i[0]))}
+        if flex: alts["S"] = (vc(o[4]) + 30, lambda q: q.activation(o[0], i[0], AF.Copy))
+        add(alts, [i], [o], tag)
+        return o
+
+    def fill(o, val, eng="V"):
+        if eng == "V": add({"V": (vc(o[4], 0.5 if wide2(o) else 1), lambda q: q.memset(o[0], val))}, [], [o], "fill")
+        else: add({"G": (130 + 2 * o[4] * CYC, lambda q: q.iota(o[0], [[0, o[4]]], int(val), 0, allow_small_or_imprecise_dtypes=True))}, [], [o], "fill")
+        return o
+
+    def gather(o, win, off, tag, eng="SV"):
+        alts = {}
+        if "S" in eng: alts["S"] = (70 + o[4] * GA * CYC, lambda q: q.activation(o[0], win[0].indirect(off[0]), AF.Copy))
+        if "V" in eng: alts["V"] = (55 + o[4] * GA * CYC, lambda q: q.tensor_copy(o[0], win[0].indirect(off[0])))
+        add(alts, [win, off], [o], tag, extra="ga")
+        return o
+
+    def compare(o, off, z, tag):
+        add({"V": (55 + o[4] * GA * CYC, lambda q: q.tensor_tensor(o[0], XS[0].indirect(off[0]), z[0], OP.is_ge))}, [XS, off, z], [o], tag, extra="ga")
+
+    def scatter(win, off, val, tag, eng):
+        alts = {}
+        if "S" in eng: alts["S"] = (70 + val[4] * SC * CYC, lambda q: q.activation(win[0].indirect(off[0]), val[0], AF.Silu))
+        if "V" in eng: alts["V"] = (55 + val[4] * SC * CYC, lambda q: q.tensor_copy(win[0].indirect(off[0]), val[0]))
+        add(alts, [off, val], [win], tag, extra="sc")
+
+    def mm(terms, tag):
+        def fn(q):
+            r = None
+            for o, l, rh, s0, s1 in terms: r = q.matmul(o[0], l[0], rh[0], s0, s1)
+            return r
+        t = sum((4 if l[1] == "cf" else 1) * max(64, rh[4]) * PEC + 5 for o, l, rh, s0, s1 in terms)
+        add({"P": (t + 60, fn)}, [x[1] for x in terms] + [x[2] for x in terms], [x[0] for x in terms], tag)
+
+    def group(o, parts):
+        return [(p[0], p[1], p[2], i == 0, i == len(parts) - 1) for i, p in enumerate(parts)]
+
+    def pick(o, mat, tile):
+        return [(o, sub(mat, 15 - r, 128), sub(tile, r, o[4], 16)) for r in range(16)]
+
+    def dma(o, i, tag, eng="Y", nbytes=0, oap=None, iap=None, twin=False):
+        oa = o[0] if oap is None else oap
+        ia = i[0] if iap is None else iap
+        add({eng: (100.0, lambda q: q.dma_start(oa, ia))}, [] if i is None else [i], [] if o is None else [o], tag, "d", nbytes)
+        if twin: ops[-1]["also"] = len(ops) - 2
+
+    def remote(o, i, tag, nbytes):
+        rid, pid, _ = topo.addr(nxt); mask = topo.mask(core, nxt)
+        add({"G": (300.0, lambda q, s: q.remote_dma(o[0], i[0], s, T.sem.sent, pid, rid, mask))}, [i], [o], tag, "r", nbytes)
+
+    def select(o, src, pat, cmp, base, cm):
+        add({"G": (170 + 2 * o[4] * CYC, lambda q: q.affine_select(o[0], src[0], pat, cmp, 0.0, base, cm))}, [src], [o], "sel")
+        return o
+
+    def scan(o, d0, d1, tag="scan"):
+        add({"V": (vc(o[4]), lambda q: q.tensor_tensor_scan(o[0], d0[0], d1[0], 0.0, OP.mult, OP.add))}, [d0, d1], [o], tag)
+        return o
+
+    def digits(v, off, tag="dig", alone=False):
+        d = B(2 * v[4]); h, l = sub(d, 0, v[4]), sub(d, v[4], v[4])
+        if alone: lin(h, v, 1.0, -64.0 if off else 0.0, tag)
+        else: ts(h, v, M64 - (OFF if off else 0.0), M64, OP.add, OP.subtract, tag)
+        tt(l, v, h, OP.subtract, tag)
+        return h, l
+
+    def spread(bank, fields, tag):
+        terms = []
+        for f, vs, plus in fields:
+            for cc in range(2):
+                o = A("px", bank * 512 + cc * 16 + f, 16, 32)
+                terms += group(o, [(o, SW[cc][gg], sub(v, gg, 16, 2)) for gg in range(2) for v in vs]
+                               + ([(o, sub(oneb, 0, 128), sub(oneb, 0, 16))] if plus else []))
+        mm(terms, tag)
+
+    def turn(o, bank, tag):
+        x = A("px", bank * 512, 512)
+        add({"V": (vc(512), lambda q: q.transpose(o[0], x[0]))}, [x], [o], tag)
+        return o
+
+    def values(o, banks, parts, tag):
+        for k, b in enumerate(banks):
+            spread(b, [(FS + d, [sub(x[d], 32 * k, 32) for x in parts], False) for d in range(2)], tag)
+            turn(sub(o, 512 * k, 512), b, tag)
+        return o
+
+    XS, WR, WW, KS = A("xs", 0, W), A("ws", 0, W), A("ws", 0, W + 2048), A("ks", 0, W)
+    NS, KI, LI = A("ns", 0, 384), A("ki", 0, 384), A("li", 0, 192)
+    dma(NS, None, "ld ns", "Y", 196608, iap=T.nsum[:])
+    dma(sub(LI, 0, 64), None, "ld rho", "Y", 32768, iap=T.rho[:])
+    dma(sub(LI, 64, 128), None, "ld nei", "Y", 65536, iap=T.nei[:])
+    D0 = A("d0", 0, C)
+    dma(D0, None, "ld d0", "Y", 262144, iap=T.dem[:, 0:C])
+    dma(KI, None, "ld kid", "Y", 196608, iap=T.kid[:])
+    dma(A("xs", 0, XA), None, "ld x", "Y", 256 * XA, iap=T.x[:, 0:XA])
+    for k in range(1, 6): ops[k]["soft"] = [k - 1]
+    oneb = fill(new("cb", 144), 1.0); onef = fill(new("cf", 128), 1.0); negb = fill(new("cb", 128), -1.0)
+    PM = [[select(new("cf", 128), onef, [[-16, 8], [BIG, 2], [-2, 8]], OP.is_equal, -q - BIG * h, 1) for h in range(2)] for q in range(2)]
+
+    def diag(name, val):
+        m = fill(new(name, 128), val)
+        return select(m, m, [[-1, 128]], OP.is_equal, 0, 1)
+
+    def rows(f0, nf):
+        m = select(new("cb", 144), oneb, [[-16, 9], [BIG, 16]], OP.is_ge, -f0 - 15 * BIG, 1)
+        return select(m, m, [[16, 9], [0, 16]], OP.is_ge, f0 + nf - 1, -1)
+    NEG, AS, AO = diag("cf", -1.0), rows(FS, 2), rows(0, 16)
+    ONE = diag("cf", 1.0)
+    NEG2, I16, I32, I128 = diag("cf", -2.0), diag("cb", -16.0), diag("cb", -32.0), diag("cb", -128.0)
+    ROT = new("cf", 128)
+    select(sub(ROT, 16, 112), sub(onef, 0, 112), [[-1, 112]], OP.is_equal, 0, 1)
+    select(sub(ROT, 0, 16), sub(onef, 0, 16), [[-1, 16]], OP.is_equal, -112, 1)
+    AK = rows(FK, 4)
+    SW = [[select(new("cb", 128), sub(oneb, 0, 128), [[-32, 4], [BIG, 2], [-1, 16]], OP.is_equal, -16 * cc - BIG * gg, 1) for gg in range(2)] for cc in range(2)]
+    AD, AB, AE, AC = rows(3, 2), rows(5, 2), rows(7, 2), rows(0, 3)
+    NO = [[select(new("cf", 128), onef, [[-32, 4], [-1, 16], [BIG, 2]], OP.is_equal, -16 * cc - BIG * q, 1) for q in range(2)] for cc in range(2)]
+    c0, c1 = A("ci", 0, 1), A("ci", 4, 1)
+    add({"G": (140.0, lambda q: q.iota(c0[0], [[0, 1]], 0, 1))}, [], [c0], "iota")
+    praw = F(96)
+    add({"G": (330.0, lambda q: q.iota(praw[0], [[16, 96]], 0, 1, allow_small_or_imprecise_dtypes=True))}, [], [praw], "iota")
+    ts(c1, c0, 112, None, OP.bitwise_and); g16 = cp(F(1), c1)
+    POS = ts(F(32), lo(praw), g16, None, OP.subtract)
+    TW = ts(F(96), praw, g16, float(W), OP.subtract, OP.add)
+    NTW = lin(F(96), TW, -1.0, 0.0); TWO = lin(F(32), sub(TW, 64, 32), 1.0, OFF)
+    P512 = lin(F(32), POS, 1.0, 512.0); P512H = [lin(F(32), POS, 1.0, 512.5), P512]
+    DIFF = [lin(F(32), POS, -1.0, -512.0), lin(F(32), POS, 1.0, -1023.0)]
+    NBASE = [lin(F(32), POS, -1.0, 0.0), lin(F(32), POS, -1.0, -1024.0)]
+    z0 = fill(A("ws", 0, 2048), 0.0); fill(A("ws", 4096, 2048), 0.0); z1 = A("ws", 2048, 2048)
+    add({"S": (vc(2048), lambda q: q.activation(z1[0], z0[0], AF.Copy))}, [z0], [z1], "fill")
+    s64, sh, sl = A("st", 0, 384), A("st", 384, 384), A("st", 768, 384)
+    ts(s64, NS, OFF, None, OP.add); ts(sh, s64, M64 - OFF, M64, OP.add, OP.subtract); tt(sl, s64, sh, OP.subtract)
+    dma(WR, sh, "w hi", "Y", 196608, oap=T.ws[FS:128:16, 0:W]); dma(None, sl, "w lo", "Y", 196608, oap=T.ws[FS + 1:128:16, 0:W], twin=True)
+    dma(A("xs", XA, W - XA), None, "ld x", "Y", 256 * (W - XA), iap=T.x[:, XA:W]); ops[-1]["soft"] = [len(ops) - 2, len(ops) - 3]
+    after = len(ops) - 1
+    fill(A("t1", HC, HC), 0, "G")
+    for k in range(3): fill(A("ks", 2048 * k, 2048), 0, "G")
+    kv, kh, kl = A("st", 1152, 384), A("sb", 0, 384), A("sb", 384, 384)
+    ts(kv, KI, -0.5, 0.5, OP.max, OP.mult); ts(kh, kv, M32, M32, OP.add, OP.subtract); tt(kl, kv, kh, OP.subtract)
+    dma(KS, kh, "k hi", "Y", 98304, oap=T.ks[FK:128:16, 0:W]); dma(None, kl, "k lo", "Y", 98304, oap=T.ks[FK + 1:128:16, 0:W], twin=True)
+    for t in range(1, RO):
+        dma(A("dz", (t - 1) * 2048 + HC, C), None, "ld dem", "Y", 262144, iap=T.dem[:, t * C:(t + 1) * C]); ops[-1]["soft"] = [after]
+    for b in range(4): cp(A("px", 512 * b, 512), A("t1", HC, HC), "fill", True)
+    lif = cp(F(192), LI)
+    S = []
+    for q in range(2):
+        p = P(2 * q, 96)
+        mm(group(p, [(p, PM[q][h], sub(lif, h, 96, 2)) for h in range(2)]), "perm")
+        ru = cp(U(96), p)
+        s = {"S1": F(192), "S2": F(192), "Ru": lo(ru), "Nu": sub(ru, 32, 64), "M": fill(B(192), 0.0), "dead": fill(B(32), 0.0)}
+        s["R"] = cp(F(32), lo(p), flex=True); cp(sub(s["S1"], 2, 64, 3), sub(p, 32, 64), flex=True)
+        s["RO"] = lin(F(32), s["R"], 1.0, OFF); s["Rd"] = digits(s["RO"], True)
+        s["z"] = cp(A("zz", q * HC, HC), sub(D0, q, HC, 2), "z0")
+        S.append(s)
+
+    def tile(h, k): return A("gt", (5 * h + k) * 1024, 1024)
+    def bias(p): return (p, negb, sub(oneb, 0, p[4]))
+    def NB(s): return sub(s["S1"], 2, 64, 3)
+    def AA(s): return sub(s["S2"], 2, 64, 3)
+    for q in range(2):
+        s = S[q]; g = gather(tile(q, 0), WR, s["Nu"], "S@n"); p = P(2 * q, 64)
+        mm(group(p, pick(p, AS, g) + [bias(p), (lo(p), NEG, s["R"]), (hi(p), NEG, s["R"])]), "x a")
+        s["Au"] = cp(U(64), p); cp(AA(s), p, flex=True)
+
+    def send_z(t, h):
+        z = S[h]["z"]; dst = A("dz", t * 2048 + 1536 * h, HC)
+        if h == 1:
+            zr = A("zr", t * HC, HC)
+            dma(zr, z, "rot", "Y", 114688, oap=T.zr[16:128, zr[2]:zr[3]], iap=T.zz[0:112, z[2]:z[3]])
+            dma(None, z, "rot", "Y", 16384, oap=T.zr[0:16, zr[2]:zr[3]], iap=T.zz[112:128, z[2]:z[3]], twin=True)
+            z = zr
+        remote(dst, z, "send z", 131072)
+
+    def walk1(t, h):
+        s = S[h]; g = gather(tile(h, 0), WR, s["Au"], "S@a%d%d" % (t, h)); p = P(2 * h, 64)
+        d = P(2 * h + 1, 64); mm(group(d, [(d, ONE, AA(s)), (d, NEG, NB(s))]), "d1")
+        cp(sub(s["S1"], 1, 64, 3), d, flex=True)
+        mm(group(p, pick(p, AS, g) + [bias(p), (p, NEG, NB(s))]), "x v3")
+        s["V3u"] = ts(U(64), p, float(W - 1), None, OP.min)
+        cp(sub(s["S2"], 1, 64, 3), tt(sub(s["S1"], 0, 64, 3), p, AA(s), OP.subtract), flex=True)
+
+    def walk2(t, h):
+        s = S[h]; g = gather(tile(h, 1), WR, s["V3u"], "S@v%d%d" % (t, h)); p = P(2 * h, 64)
+        mm(group(p, pick(p, AS, g) + [bias(p), (p, NEG2, AA(s)), (p, NEG, sub(s["S1"], 0, 64, 3))]), "x v4")
+        cp(sub(s["S2"], 0, 64, 3), p, flex=True)
+
+    def look(t, h, k, off):
+        g = tile(h, 2 + k)
+        for sd in range(2): compare(sub(g, HC * sd, HC), sub(off, 32 * sd, 32), S[h]["z"], "cmp%d%d%d" % (t, h, k))
+        return g
+
+    def looks(t, h):
+        s = S[h]; bank = 2 * h + 1; m = s["M"]; m1, m2 = sub(m, 2, 64, 3), sub(m, 1, 64, 3)
+        tri = tt(B(32), lo(AA(s)), hi(NB(s)), OP.is_equal)
+        for k, off, mk in ((0, s["Nu"], m1), (1, s["Au"], m2)):
+            g = look(t, h, k, off); p = P(bank, 64)
+            mm(group(p, pick(p, AO, g)), "x cnt")
+            ts(mk, p, 8.5, None, OP.is_lt)
+        g3 = look(t, h, 2, s["V3u"])
+        w = sub(scan(F(192), m, s["S1"]), 2, 64, 3); s["w"] = w
+        s["wu"] = ts(U(64), w, float(W - 1), None, OP.min)
+        eq = tt(B(32), lo(w), hi(w), OP.is_equal)
+        twm = P(2 * h, 64); mm(group(twm, [(twm, NEG, w), (twm, ONE, sub(TW, 0, 64))]), "twm")
+        p = P(bank, 64)
+        mm(group(p, pick(p, AO, g3) + [(p, I32, m1), (p, I32, m2), (lo(p), I16, tri), (lo(p), I128, eq), (lo(p), I128, s["dead"])]), "x cnt3")
+        a = ts(F(64), p, -55.5, None, OP.is_ge)
+        e = tt(F(32), lo(a), hi(a), OP.mult, "E%d%d" % (t, h)); s["E"] = e
+        s2 = scan(F(192), m, s["S2"]); s["a"] = sub(s2, 2, 64, 3)
+        s["prod"] = F(96)
+        for f in (lo, hi): tt(f(s["prod"]), e, f(twm), OP.mult)
+        if t < RO - 1:
+            p = P(bank, 32)
+            mm(group(p, [(p, (NEG, ROT)[h], tt(F(32), e, DIFF[h], OP.mult)), (p, NEG, NBASE[h])]), "rot")
+            oin = A("oi", (2 * t + h) * 32, 32)
+            remote(oin, cp(U(32), p), "send o", 8192)
+            if h != t % 2: ops[-1]["bonus"] = URGE
+            s["z"] = gather(A("zz", (2 * t + 2 + h) * HC, HC), A("dz", t * 2048 + HC * h, 1536), oin, "z%d%d" % (t + 1, h))
+            if t + 1 < RO - 1: send_z(t + 1, h)
+        for f in (lo, hi): tt(f(m1), f(m1), e, OP.mult)
+        s["S1"] = scan(F(192), m, s["S1"])
+        if t < RO - 1: s["S2"] = scan(F(192), m, s["S2"]); s["Nu"] = cp(U(64), NB(s))
+        else: s["S2"] = s2
+
+    def targets(s, bank, n):
+        p = P(bank, n); mm(group(p, [(p, NEG, sub(s["prod"], 0, n)), (p, NEG, sub(NTW, 0, n))]), "off")
+        s["off"] = cp(U(n), p)
+
+    def roots(h, bank, vt):
+        s = S[h]; v = lin(F(32), tt(F(32), lo(NB(s)), hi(NB(s)), OP.add), 1.0, OFF)
+        scatter(WW, s["Ru"], values(vt, [bank], [digits(v, True, alone=True)], "roots"), "W roots", WENG)
+
+    def parents(t):
+        h = t % 2; s = S[h]; w0, w1, b = lo(s["w"]), hi(s["w"]), lo(s["a"])
+        targets(s, 2 * h + 1, 64)
+        g = A("gt", 10240, 1024)
+        gather(sub(g, 0, HC), KS, lo(s["wu"]), "kid%d" % t)
+        gather(sub(g, HC, HC), WR, ts(U(32), b, float(W - 1), None, OP.min), "S@b%d" % t)
+        p = P(2 * h, 64); y, er = lo(p), hi(p)
+        mm(group(p, pick(p, AK, g) + [(y, NEG, P512H[h]), (er, NEG, w0)]), "x kid")
+        v1 = tt(F(32), y, ts(F(32), y, M1, M1, OP.add, OP.subtract), OP.is_equal)
+        yv = tt(F(32), y, tt(F(32), v1, s["E"], OP.mult), OP.mult)
+        s["ju"] = cp(U(32), tt(F(32), yv, P512, OP.add))
+        s["isb"] = tt(F(32), b, w1, OP.is_equal)
+        dr = tt(F(32), s["RO"], er, OP.subtract)
+        ev = tt(F(32), er, tt(F(32), s["isb"], dr, OP.mult), OP.add)
+        dw, da, de = digits(w0, False), digits(s["a"], False), digits(ev, True, alone=True)
+        spread(3, [(3, [dw[0]], False), (4, [dw[1]], True), (5, [lo(da[0])], False), (6, [lo(da[1])], True), (7, [de[0]], False), (8, [de[1]], False)], "T2")
+        fill(A("t2", 0, HC), 0, "G")
+        scatter(A("t2", 0, C), s["ju"], turn(A("vt", 1536, HC), 3, "T2"), "T2 %d" % t, "SV")
+        cp(A("tb", 0, HC), A("t2", 0, HC), "tb", True)
+        scatter(WW, hi(s["off"]), values(A("vt", 2048, HC), [3], [(hi(da[0]), hi(da[1])), s["Rd"]], "P1"), "W P1 %d" % t, WENG)
+
+    def children(t):
+        h = 1 - t % 2; s = S[h]; w0, w1 = lo(s["w"]), hi(s["w"])
+        p = P(2 * h, 64); tb = A("tb", 0, HC)
+        mm(group(lo(p), pick(lo(p), AB, tb)) + group(hi(p), pick(hi(p), AD, tb)), "x T2")
+        f = cp(F(64), p, flex=True); bo, wo = lo(f), hi(f)
+        xg = gather(A("gt", 11264, HC), XS, hi(s["wu"]), "x@w1")
+        kg = A("gt", 11776, HC); compare(kg, lo(s["wu"]), xg, "keep%d" % t)
+        pk = P(2 * h + 1, 32); mm(group(pk, pick(pk, AO, kg)), "x keep")
+        keep = ts(F(32), pk, 8.5, None, OP.is_ge)
+        nr = tt(F(32), ts(F(32), wo, 0.5, None, OP.is_lt), s["RO"], OP.mult)
+        p = P(2 * h, 96); bw, bq, wq, eq = sub(p, 0, 64), lo(p), hi(p), sub(p, 64, 32)
+        mm(group(eq, pick(eq, AE, tb) + [(eq, ONE, w0)]) + group(bw, [(bw, ONE, f), (bw, ONE, s["a"]), (bq, ONE, nr), (wq, ONE, nr)]), "x T2e")
+        kd = tt(F(32), keep, tt(F(32), wo, bo, OP.subtract), OP.mult)
+        kw = tt(F(32), keep, tt(F(32), w0, w1, OP.subtract), OP.mult)
+        cd = F(64); v = F(96)
+        tt(lo(cd), w1, kw, OP.add); tt(hi(cd), w0, kw, OP.subtract)
+        tt(lo(v), bq, kd, OP.add); tt(hi(v), wq, kd, OP.subtract); tt(sub(v, 64, 32), eq, kw, OP.subtract)
+        vt = values(A("vt", 0, 1536), [0, 1, 2], [digits(v, True, alone=True)], "C")
+        die = tt(F(32), ts(F(32), wo, 0.5, None, OP.is_gt), s["E"], OP.mult)
+        tt(sub(s["prod"], 64, 32), die, tt(F(32), TWO, bo, OP.subtract), OP.mult)
+        targets(s, 2 * h + 1, 96)
+        if t < RO - 1:
+            s["Au"] = cp(U(64), AA(s))
+            if AHEAD > 0: walk1(t + 1, h)
+            if AHEAD > 1: walk2(t + 1, h)
+        scatter(WW, s["off"], vt, "W C %d" % t, WENG)
+        s["dead"] = tt(B(32), s["dead"], die, OP.add)
+        dh, dl = digits(cd, False, alone=True)
+        spread(3, [(0, [lo(dh)], False), (1, [lo(dl)], False), (3, [hi(dh)], False), (4, [hi(dl)], False)], "T1")
+        spread(3, [(2, [lin(B(32), s["E"], 32768.0, 0.0)], False)], "T1 e")
+        turn(A("t1", 0, HC), 3, "T1")
+
+    def splice(t):
+        h = t % 2; s = S[h]
+        g = gather(A("gt", 12288, HC), A("t1", 0, C), s["ju"], "T1 %d" % t)
+        p = P(2 * h, 64); pc, pd = lo(p), hi(p)
+        mm(group(pc, pick(pc, AC, g) + [(pc, NEG, lo(s["a"]))]) + group(pd, pick(pd, AD, g) + [(pd, NEG, hi(s["a"]))]), "x T1")
+        s1 = ts(F(32), pc, 20000.0, None, OP.is_gt)
+        d0 = tt(F(32), s1, ts(F(32), pc, -32768.0, None, OP.add), OP.mult)
+        d1 = tt(F(32), pd, tt(F(32), s1, s["isb"], OP.mult), OP.mult)
+        tt(lo(AA(s)), lo(AA(s)), d0, OP.add); tt(hi(AA(s)), hi(AA(s)), d1, OP.add)
+        if t < RO - 1: s["Au"] = cp(U(64), AA(s))
+        s["d0"] = digits(lo(AA(s)), False)
+
+    def last_side(t, s):
+        scatter(WW, lo(s["off"]), values(A("vt", 2560, HC), [3], [s["d0"], s["Rd"]], "P0"), "W P0 %d" % t, WENG)
+
+    WENG = "S"
+    for h in range(2): send_z(0, h)
+    held = None
+    for t in range(RO):
+        e, l = t % 2, 1 - t % 2
+        if t == 0 or AHEAD < 1: walk1(t, e)
+        walk1(t, l)
+        if t == 0 or AHEAD < 2: walk2(t, e)
+        walk2(t, l)
+        if held is not None: last_side(t - 1, held)
+        looks(t, e)
+        if t == RO - 1: roots(e, 0, A("vt", 3072, HC))
+        parents(t); looks(t, l); children(t)
+        if t == RO - 1: roots(l, 3, A("vt", 3584, HC))
+        splice(t)
+        held = dict(S[e])
+    last_side(RO - 1, held)
+    live = [lin(F(32), S[q]["dead"], -1.0, 1.0) for q in range(2)]
+    for b in range(2):
+        terms = []
+        for f in range(3):
+            for cc in range(2):
+                o = A("px", b * 512 + cc * 16 + f, 16, 32)
+                terms += group(o, [(o, NO[cc][q], sub((lo(NB(S[q])), hi(NB(S[q])), live[q])[f], 16 * b, 16)) for q in range(2)])
+        mm(terms, "out")
+        turn(A("yo", 512 * b, 512), b, "out")
+    YO = A("yo", 0, 1024)
+    dma(None, YO, "yn0", "Y", 32768, oap=T.yn[:, 0:C], iap=T.yo[0:128:16, :])
+    dma(None, YO, "yn1", "Y", 32768, oap=T.yn[:, C:2 * C], iap=T.yo[1:128:16, :])
+    dma(None, YO, "yl", "Y", 32768, oap=T.yl[:], iap=T.yo[2:128:16, :])
+    dma(sh, WR, "r hi", "Y", 196608, iap=T.ws[FS:128:16, 0:W]); dma(sl, WR, "r lo", "S", 196608, iap=T.ws[FS + 1:128:16, 0:W])
+    tt(s64, sh, sl, OP.add); ts(kv, s64, M1 - OFF, M1, OP.add, OP.subtract)
+    dma(None, kv, "ys", "Y", 196608, oap=T.ys[:])
+    return ops
+
+
+def order(ops):
+    n = len(ops); hist = {}; twin = {}
+    for i, o in enumerate(ops):
+        dep = set()
+        if "also" in o:
+            twin[o["also"]] = i; dep |= ops[o["also"]]["dep"]
+        for nm, a, b in o["rd"]:
+            dep |= set(k for k, x, y, wr in hist.get(nm, []) if wr and x < b and a < y)
+        for nm, a, b in o["wr"]:
+            dep |= set(k for k, x, y, wr in hist.get(nm, []) if x < b and a < y)
+        dep |= set(twin[k] for k in dep if k in twin)
+        for nm, a, b in o["wr"]:
+            hist[nm] = [e for e in hist.get(nm, []) if not (a <= e[1] and e[2] <= b)] + [(i, a, b, True)]
+        for nm, a, b in o["rd"]: hist.setdefault(nm, []).append((i, a, b, False))
+        dep.discard(i); o["dep"] = dep
+        o["banks"] = set((nm, c // 512) for nm, a, b in o["rd"] + o["wr"] if nm in ("px", "pe") for c in (a, b - 1))
+        o["cost"] = min(v[0] for v in o["alts"].values()) + (0 if o["kind"] == "c" else 2000 + o["x"] / 200.0)
+    if "plan" not in KEPT: KEPT["plan"] = search(ops)
+    seq, eng, extra, t0, t1 = KEPT["plan"]
+    for i, o in enumerate(ops):
+        o["eng"], o["t0"], o["t1"] = eng[i], t0[i], t1[i]; o["dep"] = o["dep"] | extra[i]
+    return seq
+
+
+KEPT = {}
+
+
+def search(ops):
+    n = len(ops)
+    pred = [sorted(o["dep"] | set(o.get("soft", []))) for o in ops]
+    soft = [set(o.get("soft", [])) - o["dep"] for o in ops]
+    succ = [[] for _ in ops]
+    for i in range(n):
+        for k in pred[i]: succ[k].append(i)
+    alts = [[(e, v[0]) for e, v in o["alts"].items()] for o in ops]
+    banks = [sorted(o["banks"]) for o in ops]; comp = [o["kind"] == "c" for o in ops]; size = [o["x"] for o in ops]
+    cls = [o["cls"] for o in ops]
+
+    def plan(bonus, pen):
+        pr = [0.0] * n
+        for i in range(n - 1, -1, -1):
+            m = 0.0
+            for k in succ[i]:
+                if pr[k] > m: m = pr[k]
+            pr[i] = ops[i]["cost"] + LAT + m + bonus[i]
+        free = {"V": 0.0, "S": 0.0, "P": 0.0, "G": 0.0, "Y": 0.0}; bank = {}; pipe = 0.0
+        t0 = [0.0] * n; t1 = [0.0] * n; at = [0.0] * n; eng = [None] * n; extra = [set() for _ in range(n)]
+        left = [len(p) for p in pred]; ready = [i for i in range(n) if left[i] == 0]; seq = []
+        while ready:
+            tries = []; tmin = 1e18
+            for i in ready:
+                cand = None
+                for e, c in alts[i]:
+                    s = at[i] if at[i] > free[e] else free[e]
+                    for b in banks[i]:
+                        if b in bank and bank[b][0] != e and bank[b][1] > s: s = bank[b][1]
+                    key = s + c + (pen[i] * c if e == "V" else 0.0)
+                    if cand is None or key < cand[0]: cand = (key, s, e, c)
+                tries.append(cand)
+                if cand[1] < tmin: tmin = cand[1]
+            best = -1; tmin += SLACK
+            for j, i in enumerate(ready):
+                if tries[j][1] <= tmin and (best < 0 or pr[i] > pr[ready[best]]): best = j
+            i = ready.pop(best); _, s, e, c = tries[best]
+            eng[i] = e; t0[i] = s; free[e] = s + c
+            if comp[i]: t1[i] = s + c
+            else:
+                pipe = max(pipe, s + 1500) + size[i] / 200.0; t1[i] = pipe + 500
+            for b in banks[i]:
+                if b in bank and bank[b][0] != e: extra[i].add(bank[b][2])
+                bank[b] = (e, t1[i] + LAT, i)
+            seq.append(i)
+            for k in succ[i]:
+                r = s if i in soft[k] else t1[i] + LAT
+                if r > at[k]: at[k] = r
+                left[k] -= 1
+                if left[k] == 0: ready.append(k)
+        return seq, eng, extra, t0, t1
+
+    def replay(p, guess):
+        seq, eng, extra = p[:3]; scale, fix, lat, rate = guess
+        free = {"V": 0.0, "S": 0.0, "P": 0.0, "G": 0.0, "Y": 0.0}; t1 = [0.0] * n; pipe = 0.0
+        for i in seq:
+            e = eng[i]; s = free[e]
+            for k in ops[i]["dep"]:
+                if t1[k] + lat > s: s = t1[k] + lat
+            for k in extra[i]:
+                if t1[k] + lat > s: s = t1[k] + lat
+            c = ops[i]["alts"][e][0]
+            c = c * scale[cls[i]] + (fix if cls[i] == "small" else 0.0)
+            free[e] = s + c
+            if comp[i]: t1[i] = s + c
+            else:
+                pipe = max(pipe, s + 1500) + size[i] / rate; t1[i] = pipe + 500
+        return max(t1)
+
+    def worth(p): return max(p[4]) + sum(replay(p, gs) for gs in GUESSES)
+    state = [12345]
+
+    def rnd():
+        state[0] = (state[0] * 1103515245 + 12345) % 2147483648
+        return state[0] / 2147483648.0
+    flex = [i for i in range(n) if len(alts[i]) > 1 and alts[i][0][1] > 400]
+    bonus = [o.get("bonus", 0.0) for o in ops]; pen = [VPEN if len(a) > 1 else 0.0 for a in alts]
+    best = plan(bonus, pen); bw = worth(best)
+    for it in range(TRIES):
+        b2, p2 = list(bonus), list(pen)
+        for k in range(1 + int(3 * rnd())):
+            if rnd() < 0.3: p2[flex[int(rnd() * len(flex))]] = (0.0, 0.5, 1.5, 4.0, 50.0)[int(rnd() * 5)]
+            else: b2[int(rnd() * n)] += (rnd() - 0.4) * 8000.0
+        p = plan(b2, p2); w = worth(p)
+        if w <= bw: best, bw, bonus, pen = p, w, b2, p2
+    KEPT["worth"] = (max(best[4]), [replay(best, gs) for gs in GUESSES])
+    return best
+
+
+def rank_program(g, core, T, topo):
+    rank = T.rank_of(core)
+    if rank is None:
+        return
+    nxt = T.cores[(rank + 1) % len(T.cores)]
+    ops = build(T, topo, core, nxt)
+    seq = order(ops)
+    Q = {"V": g.vector, "S": g.scalar, "P": g.tensor, "G": g, "Y": g.sync}
+    count = {}; clock = {e: {} for e in Q}; nd = [0]; width = len(topo.engines(core, nxt))
+    for i in seq:
+        o = ops[i]; e = o["eng"]; q = Q[e]; ck = clock[e]
+        for k in sorted(o["dep"], key=lambda k: -ops[k]["t1"]):
+            sem, val = ops[k]["sig"]
+            if ck.get(sem, 0) < val:
+                q.wait_ge(T.sem[sem], val)
+                for s2, v2 in ops[k]["clock"].items(): ck[s2] = max(ck.get(s2, 0), v2)
+        fn = o["alts"][e][1]
+        if o["kind"] == "c":
+            count[e] = count.get(e, 0) + 1; o["sig"] = (e, count[e]); fn(q).then_inc(T.sem[e], 1)
+            o["clock"] = dict(ck); o["clock"][e] = count[e]
+        else:
+            sem = "q%d" % nd[0]; nd[0] += 1
+            if o["kind"] == "d":
+                fn(q).then_inc(T.sem[sem], 16); count[sem] = 16; o["clock"] = dict(ck)
+            else:
+                fn(q, T.sem[sem]); count[sem] = width; count["sent"] = count.get("sent", 0) + width; o["clock"] = {}
+            o["sig"] = (sem, count[sem]); o["clock"][sem] = count[sem]
+    for sem, val in count.items(): g.wait_ge(T.sem[sem], val)

@@ -4,6 +4,7 @@ W, C, RO, HC = 6144, 1024, 4, 512
 M64, M32, M1 = 1.5 * 2.0 ** 29, 1.5 * 2.0 ** 28, 1.5 * 2.0 ** 23
 FS, FK = 12, 10
 BIG = 1000
+KS_S = 2
 XA = 4096
 OFF = 128.0
 
@@ -24,11 +25,12 @@ SCRATCH = {
 NDMA = 44
 SEMAPHORES = ["V", "S", "P", "G", "sent"] + ["q%d" % i for i in range(NDMA)]
 
-CYC, GA, SC, FIX, LAT, PEC = 1.04, 1.56, 3.6, 40.0, 90.0, 0.6
-VPEN, SLACK, TRIES, AHEAD, URGE = 2.0, 120.0, 3500, 1, 10000.0
-GUESSES = [({"small": 1.0, "ga": 0.8, "sc": 0.6, "pe": 0.75, "o": 1.0}, -40.0, 60.0, 300.0),
-           ({"small": 1.0, "ga": 1.2, "sc": 1.5, "pe": 1.0, "o": 1.0}, -20.0, 150.0, 150.0),
-           ({"small": 1.0, "ga": 1.0, "sc": 0.8, "pe": 1.5, "o": 1.0}, 20.0, 120.0, 200.0)]
+CYC, GA, SC, FIX, LAT, PEC = 1.04, 1.56, 3.4, 5.0, 80.0, 0.52
+VPEN, SLACK, TRIES, AHEAD, URGE = 2.0, 30.0, 3800, 1, 10000.0
+GUESSES = [({"small": 1.0, "ga": a, "sc": b, "pe": c, "o": 1.0}, 0.0, d, e) for a, b, c, d, e in
+           ((0.75, 0.5, 1.0, 80.0, 300.0), (1.3, 0.5, 1.0, 80.0, 300.0), (0.75, 1.6, 1.0, 80.0, 300.0), (1.3, 1.6, 1.0, 80.0, 300.0),
+            (1.0, 1.05, 0.8, 40.0, 400.0), (1.0, 1.05, 1.27, 150.0, 200.0))]
+NORM = (145.0, 127.0, 154.0, 167.0, 187.0, 143.0, 163.0)
 
 
 def build(T, topo, core, nxt):
@@ -98,21 +100,27 @@ def build(T, topo, core, nxt):
         else: add({"G": (130 + 2 * o[4] * CYC, lambda q: q.iota(o[0], [[0, o[4]]], int(val), 0, allow_small_or_imprecise_dtypes=True))}, [], [o], "fill")
         return o
 
-    def gather(o, win, off, tag, eng="SV"):
+    mark = {}
+
+    def gather(o, win, off, tag, eng="SV", after=()):
         alts = {}
         if "S" in eng: alts["S"] = (70 + o[4] * GA * CYC, lambda q: q.activation(o[0], win[0].indirect(off[0]), AF.Copy))
         if "V" in eng: alts["V"] = (55 + o[4] * GA * CYC, lambda q: q.tensor_copy(o[0], win[0].indirect(off[0])))
-        add(alts, [win, off], [o], tag, extra="ga")
+        add(alts, [win, off] + [mark[k] for k in after if k in mark], [o], tag, extra="ga")
+        if win[1] == "ws": ops[-1]["w"] = 1
         return o
 
     def compare(o, off, z, tag):
         add({"V": (55 + o[4] * GA * CYC, lambda q: q.tensor_tensor(o[0], XS[0].indirect(off[0]), z[0], OP.is_ge))}, [XS, off, z], [o], tag, extra="ga")
 
-    def scatter(win, off, val, tag, eng):
+    def scatter(win, off, val, tag, eng, after=()):
         alts = {}
         if "S" in eng: alts["S"] = (70 + val[4] * SC * CYC, lambda q: q.activation(win[0].indirect(off[0]), val[0], AF.Silu))
         if "V" in eng: alts["V"] = (55 + val[4] * SC * CYC, lambda q: q.tensor_copy(win[0].indirect(off[0]), val[0]))
-        add(alts, [off, val], [win], tag, extra="sc")
+        if win[1] != "ws": add(alts, [off, val], [win], tag, extra="sc")
+        else:
+            add(alts, [off, val, WR] + [mark[k] for k in after if k in mark], [], tag, extra="sc")
+            mark[tag] = (None, "mark", len(mark), len(mark) + 1); ops[-1]["wr"] = [mark[tag][1:4]]; ops[-1]["w"] = 2
 
     def mm(terms, tag):
         def fn(q):
@@ -214,15 +222,19 @@ def build(T, topo, core, nxt):
     P512 = lin(F(32), POS, 1.0, 512.0); P512H = [lin(F(32), POS, 1.0, 512.5), P512]
     DIFF = [lin(F(32), POS, -1.0, -512.0), lin(F(32), POS, 1.0, -1023.0)]
     NBASE = [lin(F(32), POS, -1.0, 0.0), lin(F(32), POS, -1.0, -1024.0)]
-    z0 = fill(A("ws", 0, 2048), 0.0); fill(A("ws", 4096, 2048), 0.0); z1 = A("ws", 2048, 2048)
-    add({"S": (vc(2048), lambda q: q.activation(z1[0], z0[0], AF.Copy))}, [z0], [z1], "fill")
+    z0 = fill(A("ws", 0, 768), 0.0)
+    for k in range(1, 8):
+        if k < 4: fill(A("ws", 768 * k, 768), 0.0)
+        else: cp(A("ws", 768 * k, 768), z0, "fill", True)
     s64, sh, sl = A("st", 0, 384), A("st", 384, 384), A("st", 768, 384)
     ts(s64, NS, OFF, None, OP.add); ts(sh, s64, M64 - OFF, M64, OP.add, OP.subtract); tt(sl, s64, sh, OP.subtract)
     dma(WR, sh, "w hi", "Y", 196608, oap=T.ws[FS:128:16, 0:W]); dma(None, sl, "w lo", "Y", 196608, oap=T.ws[FS + 1:128:16, 0:W], twin=True)
     dma(A("xs", XA, W - XA), None, "ld x", "Y", 256 * (W - XA), iap=T.x[:, XA:W]); ops[-1]["soft"] = [len(ops) - 2, len(ops) - 3]
     after = len(ops) - 1
-    fill(A("t1", HC, HC), 0, "G")
-    for k in range(3): fill(A("ks", 2048 * k, 2048), 0, "G")
+    fill(A("t1", 0, C), 0.0)
+    for k in range(6):
+        if k < KS_S: cp(A("ks", C * k, C), A("t1", 0, C), "fill", True)
+        else: fill(A("ks", C * k, C), 0, "G")
     kv, kh, kl = A("st", 1152, 384), A("sb", 0, 384), A("sb", 384, 384)
     ts(kv, KI, -0.5, 0.5, OP.max, OP.mult); ts(kh, kv, M32, M32, OP.add, OP.subtract); tt(kl, kv, kh, OP.subtract)
     dma(KS, kh, "k hi", "Y", 98304, oap=T.ks[FK:128:16, 0:W]); dma(None, kl, "k lo", "Y", 98304, oap=T.ks[FK + 1:128:16, 0:W], twin=True)
@@ -260,7 +272,7 @@ def build(T, topo, core, nxt):
         remote(dst, z, "send z", 131072)
 
     def walk1(t, h):
-        s = S[h]; g = gather(tile(h, 0), WR, s["Au"], "S@a%d%d" % (t, h)); p = P(2 * h, 64)
+        s = S[h]; g = gather(tile(h, 0), WR, s["Au"], "S@a%d%d" % (t, h), after=["W C %d" % (t - 1 if h != t % 2 else t - 2)]); p = P(2 * h, 64)
         d = P(2 * h + 1, 64); mm(group(d, [(d, ONE, AA(s)), (d, NEG, NB(s))]), "d1")
         cp(sub(s["S1"], 1, 64, 3), d, flex=True)
         mm(group(p, pick(p, AS, g) + [bias(p), (p, NEG, NB(s))]), "x v3")
@@ -336,7 +348,7 @@ def build(T, topo, core, nxt):
         fill(A("t2", 0, HC), 0, "G")
         scatter(A("t2", 0, C), s["ju"], turn(A("vt", 1536, HC), 3, "T2"), "T2 %d" % t, "SV")
         cp(A("tb", 0, HC), A("t2", 0, HC), "tb", True)
-        scatter(WW, hi(s["off"]), values(A("vt", 2048, HC), [3], [(hi(da[0]), hi(da[1])), s["Rd"]], "P1"), "W P1 %d" % t, WENG)
+        scatter(WW, hi(s["off"]), values(A("vt", 2048, HC), [3], [(hi(da[0]), hi(da[1])), s["Rd"]], "P1"), "W P1 %d" % t, WENG, ["W C %d" % (t - 1)])
 
     def children(t):
         h = 1 - t % 2; s = S[h]; w0, w1 = lo(s["w"]), hi(s["w"])
@@ -352,18 +364,15 @@ def build(T, topo, core, nxt):
         mm(group(eq, pick(eq, AE, tb) + [(eq, ONE, w0)]) + group(bw, [(bw, ONE, f), (bw, ONE, s["a"]), (bq, ONE, nr), (wq, ONE, nr)]), "x T2e")
         kd = tt(F(32), keep, tt(F(32), wo, bo, OP.subtract), OP.mult)
         kw = tt(F(32), keep, tt(F(32), w0, w1, OP.subtract), OP.mult)
-        cd = F(64); v = F(96)
+        cd = P(2 * h + 1, 64); v = p
         tt(lo(cd), w1, kw, OP.add); tt(hi(cd), w0, kw, OP.subtract)
         tt(lo(v), bq, kd, OP.add); tt(hi(v), wq, kd, OP.subtract); tt(sub(v, 64, 32), eq, kw, OP.subtract)
         vt = values(A("vt", 0, 1536), [0, 1, 2], [digits(v, True, alone=True)], "C")
         die = tt(F(32), ts(F(32), wo, 0.5, None, OP.is_gt), s["E"], OP.mult)
         tt(sub(s["prod"], 64, 32), die, tt(F(32), TWO, bo, OP.subtract), OP.mult)
         targets(s, 2 * h + 1, 96)
-        if t < RO - 1:
-            s["Au"] = cp(U(64), AA(s))
-            if AHEAD > 0: walk1(t + 1, h)
-            if AHEAD > 1: walk2(t + 1, h)
-        scatter(WW, s["off"], vt, "W C %d" % t, WENG)
+        if t < RO - 1: s["Au"] = cp(U(64), AA(s))
+        scatter(WW, s["off"], vt, "W C %d" % t, WENG, ["W P1 %d" % t, "W P0 %d" % (t - 1), "W P1 %d" % (t - 1), "W C %d" % (t - 1)])
         s["dead"] = tt(B(32), s["dead"], die, OP.add)
         dh, dl = digits(cd, False, alone=True)
         spread(3, [(0, [lo(dh)], False), (1, [lo(dl)], False), (3, [hi(dh)], False), (4, [hi(dl)], False)], "T1")
@@ -383,17 +392,14 @@ def build(T, topo, core, nxt):
         s["d0"] = digits(lo(AA(s)), False)
 
     def last_side(t, s):
-        scatter(WW, lo(s["off"]), values(A("vt", 2560, HC), [3], [s["d0"], s["Rd"]], "P0"), "W P0 %d" % t, WENG)
+        scatter(WW, lo(s["off"]), values(A("vt", 2560, HC), [3], [s["d0"], s["Rd"]], "P0"), "W P0 %d" % t, WENG, ["W C %d" % (t - 1)])
 
-    WENG = "S"
+    WENG = "SV"
     for h in range(2): send_z(0, h)
     held = None
     for t in range(RO):
         e, l = t % 2, 1 - t % 2
-        if t == 0 or AHEAD < 1: walk1(t, e)
-        walk1(t, l)
-        if t == 0 or AHEAD < 2: walk2(t, e)
-        walk2(t, l)
+        walk1(t, e); walk1(t, l); walk2(t, e); walk2(t, l)
         if held is not None: last_side(t - 1, held)
         looks(t, e)
         if t == RO - 1: roots(e, 0, A("vt", 3072, HC))
@@ -415,7 +421,8 @@ def build(T, topo, core, nxt):
     dma(None, YO, "yn0", "Y", 32768, oap=T.yn[:, 0:C], iap=T.yo[0:128:16, :])
     dma(None, YO, "yn1", "Y", 32768, oap=T.yn[:, C:2 * C], iap=T.yo[1:128:16, :])
     dma(None, YO, "yl", "Y", 32768, oap=T.yl[:], iap=T.yo[2:128:16, :])
-    dma(sh, WR, "r hi", "Y", 196608, iap=T.ws[FS:128:16, 0:W]); dma(sl, WR, "r lo", "S", 196608, iap=T.ws[FS + 1:128:16, 0:W])
+    for o, f, e in ((sh, FS, "Y"), (sl, FS + 1, "S")):
+        dma(o, WR, "r", e, 196608, iap=T.ws[f:128:16, 0:W]); ops[-1]["rd"].append(("mark", 0, 99))
     tt(s64, sh, sl, OP.add); ts(kv, s64, M1 - OFF, M1, OP.add, OP.subtract)
     dma(None, kv, "ys", "Y", 196608, oap=T.ys[:])
     return ops
@@ -457,7 +464,7 @@ def search(ops):
         for k in pred[i]: succ[k].append(i)
     alts = [[(e, v[0]) for e, v in o["alts"].items()] for o in ops]
     banks = [sorted(o["banks"]) for o in ops]; comp = [o["kind"] == "c" for o in ops]; size = [o["x"] for o in ops]
-    cls = [o["cls"] for o in ops]
+    cls = [o["cls"] for o in ops]; wm = [o.get("w", 0) for o in ops]
 
     def plan(bonus, pen):
         pr = [0.0] * n
@@ -467,6 +474,7 @@ def search(ops):
                 if pr[k] > m: m = pr[k]
             pr[i] = ops[i]["cost"] + LAT + m + bonus[i]
         free = {"V": 0.0, "S": 0.0, "P": 0.0, "G": 0.0, "Y": 0.0}; bank = {}; pipe = 0.0
+        users = [-1]; wend = 0.0; wall = 0.0
         t0 = [0.0] * n; t1 = [0.0] * n; at = [0.0] * n; eng = [None] * n; extra = [set() for _ in range(n)]
         left = [len(p) for p in pred]; ready = [i for i in range(n) if left[i] == 0]; seq = []
         while ready:
@@ -477,6 +485,9 @@ def search(ops):
                     s = at[i] if at[i] > free[e] else free[e]
                     for b in banks[i]:
                         if b in bank and bank[b][0] != e and bank[b][1] > s: s = bank[b][1]
+                    if wm[i]:
+                        x = wend if wm[i] == 1 else wall
+                        if x > s: s = x
                     key = s + c + (pen[i] * c if e == "V" else 0.0)
                     if cand is None or key < cand[0]: cand = (key, s, e, c)
                 tries.append(cand)
@@ -488,10 +499,15 @@ def search(ops):
             eng[i] = e; t0[i] = s; free[e] = s + c
             if comp[i]: t1[i] = s + c
             else:
-                pipe = max(pipe, s + 1500) + size[i] / 200.0; t1[i] = pipe + 500
+                pipe = max(pipe, s + 1500) + size[i] / 300.0; t1[i] = pipe + 500
             for b in banks[i]:
                 if b in bank and bank[b][0] != e: extra[i].add(bank[b][2])
                 bank[b] = (e, t1[i] + LAT, i)
+            if wm[i]:
+                extra[i] |= set(users[:1] if wm[i] == 1 else users) - set([-1])
+                if wm[i] == 2: users = [i]; wend = t1[i] + LAT
+                else: users.append(i)
+                wall = max(wall, t1[i] + LAT)
             seq.append(i)
             for k in succ[i]:
                 r = s if i in soft[k] else t1[i] + LAT
@@ -517,7 +533,7 @@ def search(ops):
                 pipe = max(pipe, s + 1500) + size[i] / rate; t1[i] = pipe + 500
         return max(t1)
 
-    def worth(p): return max(p[4]) + sum(replay(p, gs) for gs in GUESSES)
+    def worth(p): return sum((v / w / 1000.0) ** 6 for v, w in zip([max(p[4])] + [replay(p, gs) for gs in GUESSES], NORM))
     state = [12345]
 
     def rnd():
@@ -525,15 +541,37 @@ def search(ops):
         return state[0] / 2147483648.0
     flex = [i for i in range(n) if len(alts[i]) > 1 and alts[i][0][1] > 400]
     bonus = [o.get("bonus", 0.0) for o in ops]; pen = [VPEN if len(a) > 1 else 0.0 for a in alts]
-    best = plan(bonus, pen); bw = worth(best)
+    def held_up(p):
+        seq, eng, extra, t0, t1 = p; before = {}; last = {}; out = []
+        for i in seq:
+            before[i] = last.get(eng[i], -1); last[eng[i]] = i
+        i = max(range(n), key=lambda k: t1[k])
+        while i >= 0:
+            d = max(pred[i], key=lambda k: t1[k]) if pred[i] else -1
+            if d >= 0 and t1[d] + LAT >= t0[i] - 1.0: i = d; continue
+            x = [k for k in extra[i] if t1[k] + LAT >= t0[i] - 1.0]
+            j = x[0] if x else before[i]
+            if j >= 0: out.append((i, j))
+            i = j
+        return out
+    best = plan(bonus, pen); bw = worth(best); cur, cw = best, bw; waits = held_up(best)
     for it in range(TRIES):
         b2, p2 = list(bonus), list(pen)
-        for k in range(1 + int(3 * rnd())):
-            if rnd() < 0.3: p2[flex[int(rnd() * len(flex))]] = (0.0, 0.5, 1.5, 4.0, 50.0)[int(rnd() * 5)]
+        for k in range(1 + int(2 * rnd())):
+            r = rnd()
+            if r < 0.6 and waits:
+                i, j = waits[int(rnd() * len(waits))]; r = rnd()
+                if r < 0.45: b2[i] += rnd() * 5000.0
+                elif r < 0.7: b2[j] -= rnd() * 5000.0
+                elif len(alts[j]) > 1: p2[j] = 50.0 if cur[1][j] == "V" else -0.9
+                elif len(alts[i]) > 1: p2[i] = 50.0 if cur[1][i] == "V" else -0.9
+            elif r < 0.75: p2[flex[int(rnd() * len(flex))]] = (0.0, 0.5, 1.5, 4.0, 50.0)[int(rnd() * 5)]
             else: b2[int(rnd() * n)] += (rnd() - 0.4) * 8000.0
         p = plan(b2, p2); w = worth(p)
-        if w <= bw: best, bw, bonus, pen = p, w, b2, p2
-    KEPT["worth"] = (max(best[4]), [replay(best, gs) for gs in GUESSES])
+        if w <= cw * (1.0 + 0.01 * rnd() * (1.0 - it / TRIES)):
+            cur, cw, bonus, pen = p, w, b2, p2; waits = held_up(p)
+            if w < bw: best, bw = p, w
+    KEPT["worth"] = (max(best[4]), [replay(best, gs) for gs in GUESSES + KEPT.get("more", [])])
     return best
 
 

from concourse.mybir import AluOpType as OP, ActivationFunctionType as AF

W, C, RO, HC = 6144, 1024, 4, 512
M64, M32, M1 = 1.5 * 2.0 ** 29, 1.5 * 2.0 ** 28, 1.5 * 2.0 ** 23
FS, FK = 12, 10
BIG = 1000
KS_S = 2
XA = 4096
OFF = 128.0

SCRATCH = {
    "xs": ("sbuf", [128, W], "bfloat16"), "ws": ("sbuf", [128, W + 2048], "float32"), "ks": ("sbuf", [128, W], "bfloat16"),
    "d0": ("sbuf", [128, C], "bfloat16"), "dz": ("sbuf", [128, 3 * 2048], "bfloat16"),
    "zz": ("sbuf", [128, 8 * HC], "bfloat16"), "zr": ("sbuf", [128, 3 * HC], "bfloat16"),
    "oi": ("sbuf", [128, 6 * 32], "uint16"),
    "ns": ("sbuf", [128, 384], "int32"), "ki": ("sbuf", [128, 384], "int32"), "li": ("sbuf", [128, 192], "int32"),
    "st": ("sbuf", [128, 4 * 384], "float32"), "sb": ("sbuf", [128, 2 * 384], "bfloat16"),
    "lf": ("sbuf", [128, 14848], "float32"), "lb": ("sbuf", [128, 4096], "bfloat16"), "lu": ("sbuf", [128, 3328], "uint16"),
    "gt": ("sbuf", [128, 2 * 5 * 1024 + 3072], "bfloat16"),
    "vt": ("sbuf", [128, 1536 + 5 * 512], "float32"), "t1": ("sbuf", [128, C], "float32"),
    "t2": ("sbuf", [128, C], "float32"), "tb": ("sbuf", [128, HC], "bfloat16"), "yo": ("sbuf", [128, 1024], "float32"),
    "cb": ("sbuf", [128, 2304], "bfloat16"), "cf": ("sbuf", [128, 1920], "float32"), "ci": ("sbuf", [128, 8], "int32"),
    "px": ("psum", [128, 2048], "float32"), "pe": ("psum", [128, 2048], "float32"),
}
NDMA = 44
SEMAPHORES = ["V", "S", "P", "G", "sent"] + ["q%d" % i for i in range(NDMA)]

CYC, GA, SC, FIX, LAT, PEC = 1.04, 1.56, 3.4, 5.0, 80.0, 0.52
VPEN, SLACK, TRIES, AHEAD, URGE = 2.0, 30.0, 3800, 1, 10000.0
GUESSES = [({"small": 1.0, "ga": a, "sc": b, "pe": c, "o": 1.0}, 0.0, d, e) for a, b, c, d, e in
           ((0.75, 0.5, 1.0, 80.0, 300.0), (1.3, 0.5, 1.0, 80.0, 300.0), (0.75, 1.6, 1.0, 80.0, 300.0), (1.3, 1.6, 1.0, 80.0, 300.0),
            (1.0, 1.05, 0.8, 40.0, 400.0), (1.0, 1.05, 1.27, 150.0, 200.0))]
NORM = (145.0, 127.0, 154.0, 167.0, 187.0, 143.0, 163.0)


def build(T, topo, core, nxt):
    ops = []
    top = {"lf": 0, "lb": 0, "lu": 0, "cb": 0, "cf": 0}
    ptop = [0, 0, 0, 0]

    def A(name, a, n, step=1):
        end = a + (n - 1) * step + 1
        cs = slice(a, end, step) if step > 1 else slice(a, end)
        return (T[name][0:128, cs], name, a, end, n, step)

    def sub(v, a, n, step=1):
        return A(v[1], v[2] + a * v[5], n, step * v[5])

    def new(name, n):
        a = top[name]; top[name] = a + (n + 7) // 8 * 8
        return A(name, a, n)

    def F(n): return new("lf", n)
    def B(n): return new("lb", n)
    def U(n): return new("lu", n)
    def lo(v): return sub(v, 0, 32)
    def hi(v): return sub(v, 32, 32)

    def P(bank, n):
        if ptop[bank] + n > 512: ptop[bank] = 0
        a = ptop[bank]; ptop[bank] = a + n
        return A("pe", bank * 512 + a, n)

    def add(alts, rd, wr, tag, kind="c", extra=None):
        cls = "pe" if "P" in alts else "o" if kind != "c" or "G" in alts else extra or "small"
        ops.append({"alts": alts, "rd": [v[1:4] for v in rd], "wr": [v[1:4] for v in wr], "tag": tag, "kind": kind, "x": extra, "cls": cls})

    def wide2(*vs):
        return all(v[1] in ("lb", "gt", "cb", "sb", "zz", "d0", "ks", "tb") for v in vs)

    def vc(n, k=1.0): return FIX + max(64, n * k) * CYC

    def ts(o, i, s1, s2, op0, op1=None, tag="ts"):
        rd = [i] + [s for s in (s1, s2) if isinstance(s, tuple)]
        a1 = s1[0] if isinstance(s1, tuple) else s1
        a2 = s2[0] if isinstance(s2, tuple) else s2
        if op1 is None: fn = lambda q: q.tensor_scalar(o[0], i[0], a1, None, op0)
        else: fn = lambda q: q.tensor_scalar(o[0], i[0], a1, a2, op0, op1)
        add({"V": (vc(o[4], 0.5 if wide2(o, i) else 1), fn)}, rd, [o], tag)
        return o

    def lin(o, i, scale, bias, tag="lin"):
        add({"V": (vc(o[4]), lambda q: q.tensor_scalar(o[0], i[0], scale, bias, OP.mult, OP.add)),
             "S": (vc(o[4]) + 30, lambda q: q.activation(o[0], i[0], AF.Identity, bias=bias, scale=scale))}, [i], [o], tag)
        return o

    def tt(o, a, b, op, tag="tt"):
        k = 1 if "pe" in (a[1], b[1]) else 2
        add({"V": (vc(o[4], k), lambda q: q.tensor_tensor(o[0], a[0], b[0], op))}, [a, b], [o], tag)
        return o

    def cp(o, i, tag="cp", flex=False):
        alts = {"V": (vc(o[4], 0.5 if wide2(o, i) else 1), lambda q: q.tensor_copy(o[0], i[0]))}
        if flex: alts["S"] = (vc(o[4]) + 30, lambda q: q.activation(o[0], i[0], AF.Copy))
        add(alts, [i], [o], tag)
        return o

    def fill(o, val, eng="V"):
        if eng == "V": add({"V": (vc(o[4], 0.5 if wide2(o) else 1), lambda q: q.memset(o[0], val))}, [], [o], "fill")
        else: add({"G": (130 + 2 * o[4] * CYC, lambda q: q.iota(o[0], [[0, o[4]]], int(val), 0, allow_small_or_imprecise_dtypes=True))}, [], [o], "fill")
        return o

    mark = {}

    def gather(o, win, off, tag, eng="SV", after=()):
        alts = {}
        if "S" in eng: alts["S"] = (70 + o[4] * GA * CYC, lambda q: q.activation(o[0], win[0].indirect(off[0]), AF.Copy))
        if "V" in eng: alts["V"] = (55 + o[4] * GA * CYC, lambda q: q.tensor_copy(o[0], win[0].indirect(off[0])))
        add(alts, [win, off] + [mark[k] for k in after if k in mark], [o], tag, extra="ga")
        if win[1] == "ws": ops[-1]["w"] = 1
        return o

    def compare(o, off, z, tag):
        add({"V": (55 + o[4] * GA * CYC, lambda q: q.tensor_tensor(o[0], XS[0].indirect(off[0]), z[0], OP.is_ge))}, [XS, off, z], [o], tag, extra="ga")

    def scatter(win, off, val, tag, eng, after=()):
        alts = {}
        if "S" in eng: alts["S"] = (70 + val[4] * SC * CYC, lambda q: q.activation(win[0].indirect(off[0]), val[0], AF.Silu))
        if "V" in eng: alts["V"] = (55 + val[4] * SC * CYC, lambda q: q.tensor_copy(win[0].indirect(off[0]), val[0]))
        if win[1] != "ws": add(alts, [off, val], [win], tag, extra="sc")
        else:
            add(alts, [off, val, WR] + [mark[k] for k in after if k in mark], [], tag, extra="sc")
            mark[tag] = (None, "mark", len(mark), len(mark) + 1); ops[-1]["wr"] = [mark[tag][1:4]]; ops[-1]["w"] = 2

    def mm(terms, tag):
        def fn(q):
            r = None
            for o, l, rh, s0, s1 in terms: r = q.matmul(o[0], l[0], rh[0], s0, s1)
            return r
        t = sum((4 if l[1] == "cf" else 1) * max(64, rh[4]) * PEC + 5 for o, l, rh, s0, s1 in terms)
        add({"P": (t + 60, fn)}, [x[1] for x in terms] + [x[2] for x in terms], [x[0] for x in terms], tag)

    def group(o, parts):
        return [(p[0], p[1], p[2], i == 0, i == len(parts) - 1) for i, p in enumerate(parts)]

    def pick(o, mat, tile):
        return [(o, sub(mat, 15 - r, 128), sub(tile, r, o[4], 16)) for r in range(16)]

    def dma(o, i, tag, eng="Y", nbytes=0, oap=None, iap=None, twin=False):
        oa = o[0] if oap is None else oap
        ia = i[0] if iap is None else iap
        add({eng: (100.0, lambda q: q.dma_start(oa, ia))}, [] if i is None else [i], [] if o is None else [o], tag, "d", nbytes)
        if twin: ops[-1]["also"] = len(ops) - 2

    def remote(o, i, tag, nbytes):
        rid, pid, _ = topo.addr(nxt); mask = topo.mask(core, nxt)
        add({"G": (300.0, lambda q, s: q.remote_dma(o[0], i[0], s, T.sem.sent, pid, rid, mask))}, [i], [o], tag, "r", nbytes)

    def select(o, src, pat, cmp, base, cm):
        add({"G": (170 + 2 * o[4] * CYC, lambda q: q.affine_select(o[0], src[0], pat, cmp, 0.0, base, cm))}, [src], [o], "sel")
        return o

    def scan(o, d0, d1, tag="scan"):
        add({"V": (vc(o[4]), lambda q: q.tensor_tensor_scan(o[0], d0[0], d1[0], 0.0, OP.mult, OP.add))}, [d0, d1], [o], tag)
        return o

    def digits(v, off, tag="dig", alone=False):
        d = B(2 * v[4]); h, l = sub(d, 0, v[4]), sub(d, v[4], v[4])
        if alone: lin(h, v, 1.0, -64.0 if off else 0.0, tag)
        else: ts(h, v, M64 - (OFF if off else 0.0), M64, OP.add, OP.subtract, tag)
        tt(l, v, h, OP.subtract, tag)
        return h, l

    def spread(bank, fields, tag):
        terms = []
        for f, vs, plus in fields:
            for cc in range(2):
                o = A("px", bank * 512 + cc * 16 + f, 16, 32)
                terms += group(o, [(o, SW[cc][gg], sub(v, gg, 16, 2)) for gg in range(2) for v in vs]
                               + ([(o, sub(oneb, 0, 128), sub(oneb, 0, 16))] if plus else []))
        mm(terms, tag)

    def turn(o, bank, tag):
        x = A("px", bank * 512, 512)
        add({"V": (vc(512), lambda q: q.transpose(o[0], x[0]))}, [x], [o], tag)
        return o

    def values(o, banks, parts, tag):
        for k, b in enumerate(banks):
            spread(b, [(FS + d, [sub(x[d], 32 * k, 32) for x in parts], False) for d in range(2)], tag)
            turn(sub(o, 512 * k, 512), b, tag)
        return o

    XS, WR, WW, KS = A("xs", 0, W), A("ws", 0, W), A("ws", 0, W + 2048), A("ks", 0, W)
    NS, KI, LI = A("ns", 0, 384), A("ki", 0, 384), A("li", 0, 192)
    dma(NS, None, "ld ns", "Y", 196608, iap=T.nsum[:])
    dma(sub(LI, 0, 64), None, "ld rho", "Y", 32768, iap=T.rho[:])
    dma(sub(LI, 64, 128), None, "ld nei", "Y", 65536, iap=T.nei[:])
    D0 = A("d0", 0, C)
    dma(D0, None, "ld d0", "Y", 262144, iap=T.dem[:, 0:C])
    dma(KI, None, "ld kid", "Y", 196608, iap=T.kid[:])
    dma(A("xs", 0, XA), None, "ld x", "Y", 256 * XA, iap=T.x[:, 0:XA])
    for k in range(1, 6): ops[k]["soft"] = [k - 1]
    oneb = fill(new("cb", 144), 1.0); onef = fill(new("cf", 128), 1.0); negb = fill(new("cb", 128), -1.0)
    PM = [[select(new("cf", 128), onef, [[-16, 8], [BIG, 2], [-2, 8]], OP.is_equal, -q - BIG * h, 1) for h in range(2)] for q in range(2)]

    def diag(name, val):
        m = fill(new(name, 128), val)
        return select(m, m, [[-1, 128]], OP.is_equal, 0, 1)

    def rows(f0, nf):
        m = select(new("cb", 144), oneb, [[-16, 9], [BIG, 16]], OP.is_ge, -f0 - 15 * BIG, 1)
        return select(m, m, [[16, 9], [0, 16]], OP.is_ge, f0 + nf - 1, -1)
    NEG, AS, AO = diag("cf", -1.0), rows(FS, 2), rows(0, 16)
    ONE = diag("cf", 1.0)
    NEG2, I16, I32, I128 = diag("cf", -2.0), diag("cb", -16.0), diag("cb", -32.0), diag("cb", -128.0)
    ROT = new("cf", 128)
    select(sub(ROT, 16, 112), sub(onef, 0, 112), [[-1, 112]], OP.is_equal, 0, 1)
    select(sub(ROT, 0, 16), sub(onef, 0, 16), [[-1, 16]], OP.is_equal, -112, 1)
    AK = rows(FK, 4)
    SW = [[select(new("cb", 128), sub(oneb, 0, 128), [[-32, 4], [BIG, 2], [-1, 16]], OP.is_equal, -16 * cc - BIG * gg, 1) for gg in range(2)] for cc in range(2)]
    AD, AB, AE, AC = rows(3, 2), rows(5, 2), rows(7, 2), rows(0, 3)
    NO = [[select(new("cf", 128), onef, [[-32, 4], [-1, 16], [BIG, 2]], OP.is_equal, -16 * cc - BIG * q, 1) for q in range(2)] for cc in range(2)]
    c0, c1 = A("ci", 0, 1), A("ci", 4, 1)
    add({"G": (140.0, lambda q: q.iota(c0[0], [[0, 1]], 0, 1))}, [], [c0], "iota")
    praw = F(96)
    add({"G": (330.0, lambda q: q.iota(praw[0], [[16, 96]], 0, 1, allow_small_or_imprecise_dtypes=True))}, [], [praw], "iota")
    ts(c1, c0, 112, None, OP.bitwise_and); g16 = cp(F(1), c1)
    POS = ts(F(32), lo(praw), g16, None, OP.subtract)
    TW = ts(F(96), praw, g16, float(W), OP.subtract, OP.add)
    NTW = lin(F(96), TW, -1.0, 0.0); TWO = lin(F(32), sub(TW, 64, 32), 1.0, OFF)
    P512 = lin(F(32), POS, 1.0, 512.0); P512H = [lin(F(32), POS, 1.0, 512.5), P512]
    DIFF = [lin(F(32), POS, -1.0, -512.0), lin(F(32), POS, 1.0, -1023.0)]
    NBASE = [lin(F(32), POS, -1.0, 0.0), lin(F(32), POS, -1.0, -1024.0)]
    z0 = fill(A("ws", 0, 768), 0.0)
    for k in range(1, 8):
        if k < 4: fill(A("ws", 768 * k, 768), 0.0)
        else: cp(A("ws", 768 * k, 768), z0, "fill", True)
    s64, sh, sl = A("st", 0, 384), A("st", 384, 384), A("st", 768, 384)
    ts(s64, NS, OFF, None, OP.add); ts(sh, s64, M64 - OFF, M64, OP.add, OP.subtract); tt(sl, s64, sh, OP.subtract)
    dma(WR, sh, "w hi", "Y", 196608, oap=T.ws[FS:128:16, 0:W]); dma(None, sl, "w lo", "Y", 196608, oap=T.ws[FS + 1:128:16, 0:W], twin=True)
    dma(A("xs", XA, W - XA), None, "ld x", "Y", 256 * (W - XA), iap=T.x[:, XA:W]); ops[-1]["soft"] = [len(ops) - 2, len(ops) - 3]
    after = len(ops) - 1
    fill(A("t1", 0, C), 0.0)
    for k in range(6):
        if k < KS_S: cp(A("ks", C * k, C), A("t1", 0, C), "fill", True)
        else: fill(A("ks", C * k, C), 0, "G")
    kv, kh, kl = A("st", 1152, 384), A("sb", 0, 384), A("sb", 384, 384)
    ts(kv, KI, -0.5, 0.5, OP.max, OP.mult); ts(kh, kv, M32, M32, OP.add, OP.subtract); tt(kl, kv, kh, OP.subtract)
    dma(KS, kh, "k hi", "Y", 98304, oap=T.ks[FK:128:16, 0:W]); dma(None, kl, "k lo", "Y", 98304, oap=T.ks[FK + 1:128:16, 0:W], twin=True)
    for t in range(1, RO):
        dma(A("dz", (t - 1) * 2048 + HC, C), None, "ld dem", "Y", 262144, iap=T.dem[:, t * C:(t + 1) * C]); ops[-1]["soft"] = [after]
    for b in range(4): cp(A("px", 512 * b, 512), A("t1", HC, HC), "fill", True)
    lif = cp(F(192), LI)
    S = []
    for q in range(2):
        p = P(2 * q, 96)
        mm(group(p, [(p, PM[q][h], sub(lif, h, 96, 2)) for h in range(2)]), "perm")
        ru = cp(U(96), p)
        s = {"S1": F(192), "S2": F(192), "Ru": lo(ru), "Nu": sub(ru, 32, 64), "M": fill(B(192), 0.0), "dead": fill(B(32), 0.0)}
        s["R"] = cp(F(32), lo(p), flex=True); cp(sub(s["S1"], 2, 64, 3), sub(p, 32, 64), flex=True)
        s["RO"] = lin(F(32), s["R"], 1.0, OFF); s["Rd"] = digits(s["RO"], True)
        s["z"] = cp(A("zz", q * HC, HC), sub(D0, q, HC, 2), "z0")
        S.append(s)

    def tile(h, k): return A("gt", (5 * h + k) * 1024, 1024)
    def bias(p): return (p, negb, sub(oneb, 0, p[4]))
    def NB(s): return sub(s["S1"], 2, 64, 3)
    def AA(s): return sub(s["S2"], 2, 64, 3)
    for q in range(2):
        s = S[q]; g = gather(tile(q, 0), WR, s["Nu"], "S@n"); p = P(2 * q, 64)
        mm(group(p, pick(p, AS, g) + [bias(p), (lo(p), NEG, s["R"]), (hi(p), NEG, s["R"])]), "x a")
        s["Au"] = cp(U(64), p); cp(AA(s), p, flex=True)

    def send_z(t, h):
        z = S[h]["z"]; dst = A("dz", t * 2048 + 1536 * h, HC)
        if h == 1:
            zr = A("zr", t * HC, HC)
            dma(zr, z, "rot", "Y", 114688, oap=T.zr[16:128, zr[2]:zr[3]], iap=T.zz[0:112, z[2]:z[3]])
            dma(None, z, "rot", "Y", 16384, oap=T.zr[0:16, zr[2]:zr[3]], iap=T.zz[112:128, z[2]:z[3]], twin=True)
            z = zr
        remote(dst, z, "send z", 131072)

    def walk1(t, h):
        s = S[h]; g = gather(tile(h, 0), WR, s["Au"], "S@a%d%d" % (t, h), after=["W C %d" % (t - 1 if h != t % 2 else t - 2)]); p = P(2 * h, 64)
        d = P(2 * h + 1, 64); mm(group(d, [(d, ONE, AA(s)), (d, NEG, NB(s))]), "d1")
        cp(sub(s["S1"], 1, 64, 3), d, flex=True)
        mm(group(p, pick(p, AS, g) + [bias(p), (p, NEG, NB(s))]), "x v3")
        s["V3u"] = ts(U(64), p, float(W - 1), None, OP.min)
        cp(sub(s["S2"], 1, 64, 3), tt(sub(s["S1"], 0, 64, 3), p, AA(s), OP.subtract), flex=True)

    def walk2(t, h):
        s = S[h]; g = gather(tile(h, 1), WR, s["V3u"], "S@v%d%d" % (t, h)); p = P(2 * h, 64)
        mm(group(p, pick(p, AS, g) + [bias(p), (p, NEG2, AA(s)), (p, NEG, sub(s["S1"], 0, 64, 3))]), "x v4")
        cp(sub(s["S2"], 0, 64, 3), p, flex=True)

    def look(t, h, k, off):
        g = tile(h, 2 + k)
        for sd in range(2): compare(sub(g, HC * sd, HC), sub(off, 32 * sd, 32), S[h]["z"], "cmp%d%d%d" % (t, h, k))
        return g

    def looks(t, h):
        s = S[h]; bank = 2 * h + 1; m = s["M"]; m1, m2 = sub(m, 2, 64, 3), sub(m, 1, 64, 3)
        tri = tt(B(32), lo(AA(s)), hi(NB(s)), OP.is_equal)
        for k, off, mk in ((0, s["Nu"], m1), (1, s["Au"], m2)):
            g = look(t, h, k, off); p = P(bank, 64)
            mm(group(p, pick(p, AO, g)), "x cnt")
            ts(mk, p, 8.5, None, OP.is_lt)
        g3 = look(t, h, 2, s["V3u"])
        w = sub(scan(F(192), m, s["S1"]), 2, 64, 3); s["w"] = w
        s["wu"] = ts(U(64), w, float(W - 1), None, OP.min)
        eq = tt(B(32), lo(w), hi(w), OP.is_equal)
        twm = P(2 * h, 64); mm(group(twm, [(twm, NEG, w), (twm, ONE, sub(TW, 0, 64))]), "twm")
        p = P(bank, 64)
        mm(group(p, pick(p, AO, g3) + [(p, I32, m1), (p, I32, m2), (lo(p), I16, tri), (lo(p), I128, eq), (lo(p), I128, s["dead"])]), "x cnt3")
        a = ts(F(64), p, -55.5, None, OP.is_ge)
        e = tt(F(32), lo(a), hi(a), OP.mult, "E%d%d" % (t, h)); s["E"] = e
        s2 = scan(F(192), m, s["S2"]); s["a"] = sub(s2, 2, 64, 3)
        s["prod"] = F(96)
        for f in (lo, hi): tt(f(s["prod"]), e, f(twm), OP.mult)
        if t < RO - 1:
            p = P(bank, 32)
            mm(group(p, [(p, (NEG, ROT)[h], tt(F(32), e, DIFF[h], OP.mult)), (p, NEG, NBASE[h])]), "rot")
            oin = A("oi", (2 * t + h) * 32, 32)
            remote(oin, cp(U(32), p), "send o", 8192)
            if h != t % 2: ops[-1]["bonus"] = URGE
            s["z"] = gather(A("zz", (2 * t + 2 + h) * HC, HC), A("dz", t * 2048 + HC * h, 1536), oin, "z%d%d" % (t + 1, h))
            if t + 1 < RO - 1: send_z(t + 1, h)
        for f in (lo, hi): tt(f(m1), f(m1), e, OP.mult)
        s["S1"] = scan(F(192), m, s["S1"])
        if t < RO - 1: s["S2"] = scan(F(192), m, s["S2"]); s["Nu"] = cp(U(64), NB(s))
        else: s["S2"] = s2

    def targets(s, bank, n):
        p = P(bank, n); mm(group(p, [(p, NEG, sub(s["prod"], 0, n)), (p, NEG, sub(NTW, 0, n))]), "off")
        s["off"] = cp(U(n), p)

    def roots(h, bank, vt):
        s = S[h]; v = lin(F(32), tt(F(32), lo(NB(s)), hi(NB(s)), OP.add), 1.0, OFF)
        scatter(WW, s["Ru"], values(vt, [bank], [digits(v, True, alone=True)], "roots"), "W roots", WENG)

    def parents(t):
        h = t % 2; s = S[h]; w0, w1, b = lo(s["w"]), hi(s["w"]), lo(s["a"])
        targets(s, 2 * h + 1, 64)
        g = A("gt", 10240, 1024)
        gather(sub(g, 0, HC), KS, lo(s["wu"]), "kid%d" % t)
        gather(sub(g, HC, HC), WR, ts(U(32), b, float(W - 1), None, OP.min), "S@b%d" % t)
        p = P(2 * h, 64); y, er = lo(p), hi(p)
        mm(group(p, pick(p, AK, g) + [(y, NEG, P512H[h]), (er, NEG, w0)]), "x kid")
        v1 = tt(F(32), y, ts(F(32), y, M1, M1, OP.add, OP.subtract), OP.is_equal)
        yv = tt(F(32), y, tt(F(32), v1, s["E"], OP.mult), OP.mult)
        s["ju"] = cp(U(32), tt(F(32), yv, P512, OP.add))
        s["isb"] = tt(F(32), b, w1, OP.is_equal)
        dr = tt(F(32), s["RO"], er, OP.subtract)
        ev = tt(F(32), er, tt(F(32), s["isb"], dr, OP.mult), OP.add)
        dw, da, de = digits(w0, False), digits(s["a"], False), digits(ev, True, alone=True)
        spread(3, [(3, [dw[0]], False), (4, [dw[1]], True), (5, [lo(da[0])], False), (6, [lo(da[1])], True), (7, [de[0]], False), (8, [de[1]], False)], "T2")
        fill(A("t2", 0, HC), 0, "G")
        scatter(A("t2", 0, C), s["ju"], turn(A("vt", 1536, HC), 3, "T2"), "T2 %d" % t, "SV")
        cp(A("tb", 0, HC), A("t2", 0, HC), "tb", True)
        scatter(WW, hi(s["off"]), values(A("vt", 2048, HC), [3], [(hi(da[0]), hi(da[1])), s["Rd"]], "P1"), "W P1 %d" % t, WENG, ["W C %d" % (t - 1)])

    def children(t):
        h = 1 - t % 2; s = S[h]; w0, w1 = lo(s["w"]), hi(s["w"])
        p = P(2 * h, 64); tb = A("tb", 0, HC)
        mm(group(lo(p), pick(lo(p), AB, tb)) + group(hi(p), pick(hi(p), AD, tb)), "x T2")
        f = cp(F(64), p, flex=True); bo, wo = lo(f), hi(f)
        xg = gather(A("gt", 11264, HC), XS, hi(s["wu"]), "x@w1")
        kg = A("gt", 11776, HC); compare(kg, lo(s["wu"]), xg, "keep%d" % t)
        pk = P(2 * h + 1, 32); mm(group(pk, pick(pk, AO, kg)), "x keep")
        keep = ts(F(32), pk, 8.5, None, OP.is_ge)
        nr = tt(F(32), ts(F(32), wo, 0.5, None, OP.is_lt), s["RO"], OP.mult)
        p = P(2 * h, 96); bw, bq, wq, eq = sub(p, 0, 64), lo(p), hi(p), sub(p, 64, 32)
        mm(group(eq, pick(eq, AE, tb) + [(eq, ONE, w0)]) + group(bw, [(bw, ONE, f), (bw, ONE, s["a"]), (bq, ONE, nr), (wq, ONE, nr)]), "x T2e")
        kd = tt(F(32), keep, tt(F(32), wo, bo, OP.subtract), OP.mult)
        kw = tt(F(32), keep, tt(F(32), w0, w1, OP.subtract), OP.mult)
        cd = P(2 * h + 1, 64); v = p
        tt(lo(cd), w1, kw, OP.add); tt(hi(cd), w0, kw, OP.subtract)
        tt(lo(v), bq, kd, OP.add); tt(hi(v), wq, kd, OP.subtract); tt(sub(v, 64, 32), eq, kw, OP.subtract)
        vt = values(A("vt", 0, 1536), [0, 1, 2], [digits(v, True, alone=True)], "C")
        die = tt(F(32), ts(F(32), wo, 0.5, None, OP.is_gt), s["E"], OP.mult)
        tt(sub(s["prod"], 64, 32), die, tt(F(32), TWO, bo, OP.subtract), OP.mult)
        targets(s, 2 * h + 1, 96)
        if t < RO - 1: s["Au"] = cp(U(64), AA(s))
        scatter(WW, s["off"], vt, "W C %d" % t, WENG, ["W P1 %d" % t, "W P0 %d" % (t - 1), "W P1 %d" % (t - 1), "W C %d" % (t - 1)])
        s["dead"] = tt(B(32), s["dead"], die, OP.add)
        dh, dl = digits(cd, False, alone=True)
        spread(3, [(0, [lo(dh)], False), (1, [lo(dl)], False), (3, [hi(dh)], False), (4, [hi(dl)], False)], "T1")
        spread(3, [(2, [lin(B(32), s["E"], 32768.0, 0.0)], False)], "T1 e")
        turn(A("t1", 0, HC), 3, "T1")

    def splice(t):
        h = t % 2; s = S[h]
        g = gather(A("gt", 12288, HC), A("t1", 0, C), s["ju"], "T1 %d" % t)
        p = P(2 * h, 64); pc, pd = lo(p), hi(p)
        mm(group(pc, pick(pc, AC, g) + [(pc, NEG, lo(s["a"]))]) + group(pd, pick(pd, AD, g) + [(pd, NEG, hi(s["a"]))]), "x T1")
        s1 = ts(F(32), pc, 20000.0, None, OP.is_gt)
        d0 = tt(F(32), s1, ts(F(32), pc, -32768.0, None, OP.add), OP.mult)
        d1 = tt(F(32), pd, tt(F(32), s1, s["isb"], OP.mult), OP.mult)
        tt(lo(AA(s)), lo(AA(s)), d0, OP.add); tt(hi(AA(s)), hi(AA(s)), d1, OP.add)
        if t < RO - 1: s["Au"] = cp(U(64), AA(s))
        s["d0"] = digits(lo(AA(s)), False)

    def last_side(t, s):
        scatter(WW, lo(s["off"]), values(A("vt", 2560, HC), [3], [s["d0"], s["Rd"]], "P0"), "W P0 %d" % t, WENG, ["W C %d" % (t - 1)])

    WENG = "SV"
    for h in range(2): send_z(0, h)
    held = None
    for t in range(RO):
        e, l = t % 2, 1 - t % 2
        walk1(t, e); walk1(t, l); walk2(t, e); walk2(t, l)
        if held is not None: last_side(t - 1, held)
        looks(t, e)
        if t == RO - 1: roots(e, 0, A("vt", 3072, HC))
        parents(t); looks(t, l); children(t)
        if t == RO - 1: roots(l, 3, A("vt", 3584, HC))
        splice(t)
        held = dict(S[e])
    last_side(RO - 1, held)
    live = [lin(F(32), S[q]["dead"], -1.0, 1.0) for q in range(2)]
    for b in range(2):
        terms = []
        for f in range(3):
            for cc in range(2):
                o = A("px", b * 512 + cc * 16 + f, 16, 32)
                terms += group(o, [(o, NO[cc][q], sub((lo(NB(S[q])), hi(NB(S[q])), live[q])[f], 16 * b, 16)) for q in range(2)])
        mm(terms, "out")
        turn(A("yo", 512 * b, 512), b, "out")
    YO = A("yo", 0, 1024)
    dma(None, YO, "yn0", "Y", 32768, oap=T.yn[:, 0:C], iap=T.yo[0:128:16, :])
    dma(None, YO, "yn1", "Y", 32768, oap=T.yn[:, C:2 * C], iap=T.yo[1:128:16, :])
    dma(None, YO, "yl", "Y", 32768, oap=T.yl[:], iap=T.yo[2:128:16, :])
    for o, f, e in ((sh, FS, "Y"), (sl, FS + 1, "S")):
        dma(o, WR, "r", e, 196608, iap=T.ws[f:128:16, 0:W]); ops[-1]["rd"].append(("mark", 0, 99))
    tt(s64, sh, sl, OP.add); ts(kv, s64, M1 - OFF, M1, OP.add, OP.subtract)
    dma(None, kv, "ys", "Y", 196608, oap=T.ys[:])
    return ops


def order(ops):
    n = len(ops); hist = {}; twin = {}
    for i, o in enumerate(ops):
        dep = set()
        if "also" in o:
            twin[o["also"]] = i; dep |= ops[o["also"]]["dep"]
        for nm, a, b in o["rd"]:
            dep |= set(k for k, x, y, wr in hist.get(nm, []) if wr and x < b and a < y)
        for nm, a, b in o["wr"]:
            dep |= set(k for k, x, y, wr in hist.get(nm, []) if x < b and a < y)
        dep |= set(twin[k] for k in dep if k in twin)
        for nm, a, b in o["wr"]:
            hist[nm] = [e for e in hist.get(nm, []) if not (a <= e[1] and e[2] <= b)] + [(i, a, b, True)]
        for nm, a, b in o["rd"]: hist.setdefault(nm, []).append((i, a, b, False))
        dep.discard(i); o["dep"] = dep
        o["banks"] = set((nm, c // 512) for nm, a, b in o["rd"] + o["wr"] if nm in ("px", "pe") for c in (a, b - 1))
        o["cost"] = min(v[0] for v in o["alts"].values()) + (0 if o["kind"] == "c" else 2000 + o["x"] / 200.0)
    if "plan" not in KEPT: KEPT["plan"] = search(ops)
    seq, eng, extra, t0, t1 = KEPT["plan"]
    for i, o in enumerate(ops):
        o["eng"], o["t0"], o["t1"] = eng[i], t0[i], t1[i]; o["dep"] = o["dep"] | extra[i]
    return seq


KEPT = {}


def search(ops):
    n = len(ops)
    pred = [sorted(o["dep"] | set(o.get("soft", []))) for o in ops]
    soft = [set(o.get("soft", [])) - o["dep"] for o in ops]
    succ = [[] for _ in ops]
    for i in range(n):
        for k in pred[i]: succ[k].append(i)
    alts = [[(e, v[0]) for e, v in o["alts"].items()] for o in ops]
    banks = [sorted(o["banks"]) for o in ops]; comp = [o["kind"] == "c" for o in ops]; size = [o["x"] for o in ops]
    cls = [o["cls"] for o in ops]; wm = [o.get("w", 0) for o in ops]

    def plan(bonus, pen):
        pr = [0.0] * n
        for i in range(n - 1, -1, -1):
            m = 0.0
            for k in succ[i]:
                if pr[k] > m: m = pr[k]
            pr[i] = ops[i]["cost"] + LAT + m + bonus[i]
        free = {"V": 0.0, "S": 0.0, "P": 0.0, "G": 0.0, "Y": 0.0}; bank = {}; pipe = 0.0
        users = [-1]; wend = 0.0; wall = 0.0
        t0 = [0.0] * n; t1 = [0.0] * n; at = [0.0] * n; eng = [None] * n; extra = [set() for _ in range(n)]
        left = [len(p) for p in pred]; ready = [i for i in range(n) if left[i] == 0]; seq = []
        while ready:
            tries = []; tmin = 1e18
            for i in ready:
                cand = None
                for e, c in alts[i]:
                    s = at[i] if at[i] > free[e] else free[e]
                    for b in banks[i]:
                        if b in bank and bank[b][0] != e and bank[b][1] > s: s = bank[b][1]
                    if wm[i]:
                        x = wend if wm[i] == 1 else wall
                        if x > s: s = x
                    key = s + c + (pen[i] * c if e == "V" else 0.0)
                    if cand is None or key < cand[0]: cand = (key, s, e, c)
                tries.append(cand)
                if cand[1] < tmin: tmin = cand[1]
            best = -1; tmin += SLACK
            for j, i in enumerate(ready):
                if tries[j][1] <= tmin and (best < 0 or pr[i] > pr[ready[best]]): best = j
            i = ready.pop(best); _, s, e, c = tries[best]
            eng[i] = e; t0[i] = s; free[e] = s + c
            if comp[i]: t1[i] = s + c
            else:
                pipe = max(pipe, s + 1500) + size[i] / 300.0; t1[i] = pipe + 500
            for b in banks[i]:
                if b in bank and bank[b][0] != e: extra[i].add(bank[b][2])
                bank[b] = (e, t1[i] + LAT, i)
            if wm[i]:
                extra[i] |= set(users[:1] if wm[i] == 1 else users) - set([-1])
                if wm[i] == 2: users = [i]; wend = t1[i] + LAT
                else: users.append(i)
                wall = max(wall, t1[i] + LAT)
            seq.append(i)
            for k in succ[i]:
                r = s if i in soft[k] else t1[i] + LAT
                if r > at[k]: at[k] = r
                left[k] -= 1
                if left[k] == 0: ready.append(k)
        return seq, eng, extra, t0, t1

    def replay(p, guess):
        seq, eng, extra = p[:3]; scale, fix, lat, rate = guess
        free = {"V": 0.0, "S": 0.0, "P": 0.0, "G": 0.0, "Y": 0.0}; t1 = [0.0] * n; pipe = 0.0
        for i in seq:
            e = eng[i]; s = free[e]
            for k in ops[i]["dep"]:
                if t1[k] + lat > s: s = t1[k] + lat
            for k in extra[i]:
                if t1[k] + lat > s: s = t1[k] + lat
            c = ops[i]["alts"][e][0]
            c = c * scale[cls[i]] + (fix if cls[i] == "small" else 0.0)
            free[e] = s + c
            if comp[i]: t1[i] = s + c
            else:
                pipe = max(pipe, s + 1500) + size[i] / rate; t1[i] = pipe + 500
        return max(t1)

    def worth(p): return sum((v / w / 1000.0) ** 6 for v, w in zip([max(p[4])] + [replay(p, gs) for gs in GUESSES], NORM))
    state = [12345]

    def rnd():
        state[0] = (state[0] * 1103515245 + 12345) % 2147483648
        return state[0] / 2147483648.0
    flex = [i for i in range(n) if len(alts[i]) > 1 and alts[i][0][1] > 400]
    bonus = [o.get("bonus", 0.0) for o in ops]; pen = [VPEN if len(a) > 1 else 0.0 for a in alts]
    def held_up(p):
        seq, eng, extra, t0, t1 = p; before = {}; last = {}; out = []
        for i in seq:
            before[i] = last.get(eng[i], -1); last[eng[i]] = i
        i = max(range(n), key=lambda k: t1[k])
        while i >= 0:
            d = max(pred[i], key=lambda k: t1[k]) if pred[i] else -1
            if d >= 0 and t1[d] + LAT >= t0[i] - 1.0: i = d; continue
            x = [k for k in extra[i] if t1[k] + LAT >= t0[i] - 1.0]
            j = x[0] if x else before[i]
            if j >= 0: out.append((i, j))
            i = j
        return out
    best = plan(bonus, pen); bw = worth(best); cur, cw = best, bw; waits = held_up(best)
    for it in range(TRIES):
        b2, p2 = list(bonus), list(pen)
        for k in range(1 + int(2 * rnd())):
            r = rnd()
            if r < 0.6 and waits:
                i, j = waits[int(rnd() * len(waits))]; r = rnd()
                if r < 0.45: b2[i] += rnd() * 5000.0
                elif r < 0.7: b2[j] -= rnd() * 5000.0
                elif len(alts[j]) > 1: p2[j] = 50.0 if cur[1][j] == "V" else -0.9
                elif len(alts[i]) > 1: p2[i] = 50.0 if cur[1][i] == "V" else -0.9
            elif r < 0.75: p2[flex[int(rnd() * len(flex))]] = (0.0, 0.5, 1.5, 4.0, 50.0)[int(rnd() * 5)]
            else: b2[int(rnd() * n)] += (rnd() - 0.4) * 8000.0
        p = plan(b2, p2); w = worth(p)
        if w <= cw * (1.0 + 0.01 * rnd() * (1.0 - it / TRIES)):
            cur, cw, bonus, pen = p, w, b2, p2; waits = held_up(p)
            if w < bw: best, bw = p, w
    KEPT["worth"] = (max(best[4]), [replay(best, gs) for gs in GUESSES + KEPT.get("more", [])])
    return best


def rank_program(g, core, T, topo):
    rank = T.rank_of(core)
    if rank is None:
        return
    nxt = T.cores[(rank + 1) % len(T.cores)]
    ops = build(T, topo, core, nxt)
    seq = order(ops)
    Q = {"V": g.vector, "S": g.scalar, "P": g.tensor, "G": g, "Y": g.sync}
    count = {}; clock = {e: {} for e in Q}; nd = [0]; width = len(topo.engines(core, nxt))
    for i in seq:
        o = ops[i]; e = o["eng"]; q = Q[e]; ck = clock[e]
        for k in sorted(o["dep"], key=lambda k: -ops[k]["t1"]):
            sem, val = ops[k]["sig"]
            if ck.get(sem, 0) < val:
                q.wait_ge(T.sem[sem], val)
                for s2, v2 in ops[k]["clock"].items(): ck[s2] = max(ck.get(s2, 0), v2)
        fn = o["alts"][e][1]
        if o["kind"] == "c":
            count[e] = count.get(e, 0) + 1; o["sig"] = (e, count[e]); fn(q).then_inc(T.sem[e], 1)
            o["clock"] = dict(ck); o["clock"][e] = count[e]
        else:
            sem = "q%d" % nd[0]; nd[0] += 1
            if o["kind"] == "d":
                fn(q).then_inc(T.sem[sem], 16); count[sem] = 16; o["clock"] = dict(ck)
            else:
                fn(q, T.sem[sem]); count[sem] = width; count["sent"] = count.get("sent", 0) + width; o["clock"] = {}
            o["sig"] = (sem, count[sem]); o["clock"][sem] = count[sem]
    for sem, val in count.items(): g.wait_ge(T.sem[sem], val)
